import numpy as np
import ml_dtypes


def mxq(x, axis, fmt="e4m3"):
    dtype, down = {"e4m3": (ml_dtypes.float8_e4m3fn, 7), "e5m2": (ml_dtypes.float8_e5m2, 14)}[fmt]
    v = np.moveaxis(np.asarray(x, np.float32).astype(ml_dtypes.bfloat16).astype(np.float64), axis, -1)
    blocks = v.reshape(v.shape[:-1] + (-1, 32))
    amax = np.abs(blocks).max(-1, keepdims=True)
    byte = np.maximum(np.where(amax > 0, np.frexp(amax)[1] - 1 + 127, 0) - down, 1)
    scale = np.exp2(byte - 127.0)
    codes = (blocks / scale).astype(np.float32).astype(dtype).astype(np.float64)
    return np.moveaxis((codes * scale).reshape(v.shape), -1, axis)


WIDE = False


def mx_kscale(k):
    if not WIDE:
        return np.ones(k)
    levels = np.array([10, -10, 5, -5, 0])
    if k % 512:
        return np.exp2(np.random.permutation(np.resize(levels, k // 32))).repeat(32)
    a = np.empty((k // 512, 16))
    for p in range(k // 512):
        a[p, :8] = np.random.permutation(np.resize(levels, 8))
        for g in range(8):
            far = levels[np.abs(levels - a[p, g]) >= 10]
            a[p, g + 8] = far[np.random.randint(len(far))]
    return np.exp2(a.ravel()).repeat(32)


BF16 = ml_dtypes.bfloat16


def bf(x):
    return np.asarray(x, np.float32).astype(BF16)


def f64(x):
    return np.asarray(x).astype(np.float64)


T, D, DS, F = 1024, 1024, 1024, 1024


def sigmoid(v):
    return 1.0 / (1.0 + np.exp(-v))


def draw0():
    s, r, t = mx_kscale(D), mx_kscale(DS), mx_kscale(F)
    return {
        "k_recv": bf(np.random.standard_normal((T, D)) * s),
        "k_share": bf(np.random.standard_normal((T, DS)) * r),
        "w_recv": bf(np.random.standard_normal((D, F)) / np.sqrt(D) / s[:, None]),
        "w_share": bf(np.random.standard_normal((DS, F)) / np.sqrt(DS) / r[:, None]),
        "g_hid": bf((1.0 + 0.1 * np.random.standard_normal(F)) * t),
        "w_delta": bf(np.random.standard_normal((F, D)) * 2.0 / np.sqrt(F) / t[:, None] * s),
        "w_gate": bf(np.random.standard_normal((F, D)) * 1.5 / np.sqrt(F) / t[:, None]),
    }


def core(k_recv, k_share, w_recv, w_share, g_hid, w_delta, w_gate):
    kr = f64(k_recv)
    u = (mxq(kr, 1, "e4m3") @ mxq(f64(w_recv), 0, "e4m3")) + (mxq(f64(k_share), 1, "e4m3") @ mxq(f64(w_share), 0, "e4m3"))
    h = u * sigmoid(u) * f64(g_hid)[None, :]
    hq = mxq(h, 1, "e4m3")
    delta = hq @ mxq(f64(w_delta), 0, "e4m3")
    gate = sigmoid(hq @ mxq(f64(w_gate), 0, "e4m3"))
    return kr + gate * delta


def e4m3fn_bytes(y):
    return np.clip(np.asarray(y, np.float64), -448.0, 448.0).astype(np.float32).astype(ml_dtypes.float8_e4m3fn).view(np.uint8)


def e4m3fn_values(b):
    return np.asarray(b, np.uint8).view(ml_dtypes.float8_e4m3fn).astype(np.float64)


def setup_inputs():
    d = draw0()
    x0 = np.asarray(d['w_share']).astype(np.float64)
    s = (np.max(np.abs(x0), axis=(1,), keepdims=True) / 448.0).astype(np.float32)
    out = {}
    for k, v in d.items():
        if k == 'w_share':
            out['w_share_bytes'] = e4m3fn_bytes(x0 / s.astype(np.float64))
            out['w_share_scale'] = s
        else:
            out[k] = v
    return out


def reference(k_recv, k_share, w_recv, w_share_bytes, w_share_scale, g_hid, w_delta, w_gate):
    return core(k_recv, k_share, w_recv, e4m3fn_values(w_share_bytes) * w_share_scale.astype(np.float64), g_hid, w_delta, w_gate)

@@ -1,0 +1,369 @@
+from contextlib import ExitStack
+
+import concourse.mybir as mybir
+from concourse.masks import make_identity
+
+T, D, DS, F = 1024, 1024, 1024, 1024
+FLOPS = 2 * T * F * (D + DS) + 2 * 2 * T * F * D
+
+P = 128
+F32 = mybir.dt.float32
+BF16 = mybir.dt.bfloat16
+U32 = mybir.dt.uint32
+U8 = mybir.dt.uint8
+FP8 = mybir.dt.float8_e4m3fn
+FP8X4 = mybir.dt.float8_e4m3fn_x4
+ACT = mybir.ActivationFunctionType
+ALU = mybir.AluOpType
+
+
+def tile_cachetocachegatedkeyfuser_kernel(
+    tc, k_recv, k_share, w_recv, w_share_bytes, w_share_scale, g_hid, w_delta, w_gate, out
+):
+    nc = tc.nc
+    with ExitStack() as ctx:
+        keep = ctx.enter_context(tc.tile_pool(name="keep", bufs=1))
+        wrawp = ctx.enter_context(tc.tile_pool(name="wrawp", bufs=7))
+        widep = ctx.enter_context(tc.tile_pool(name="widep", bufs=3))
+        wgrpp = ctx.enter_context(tc.tile_pool(name="wgrpp", bufs=4))
+        kgrpp = ctx.enter_context(tc.tile_pool(name="kgrpp", bufs=3))
+        hidp = ctx.enter_context(tc.tile_pool(name="hidp", bufs=2))
+        outp = ctx.enter_context(tc.tile_pool(name="outp", bufs=4))
+        psum = ctx.enter_context(tc.psum_pool(name="psum", bufs=8))
+
+        k_view = {
+            "r": k_recv.rearrange("(h b r) (c k) -> h c r b k", b=4, r=P, c=2),
+            "s": k_share.rearrange("(h b r) (c k) -> h c r b k", b=4, r=P, c=2),
+        }
+        w_view = {
+            "r": w_recv.rearrange("(c p j) (g n) -> c g p j n", p=P, j=4, g=2),
+            "d": w_delta.rearrange("(c p j) (g n) -> c g p j n", p=P, j=4, g=2),
+            "g": w_gate.rearrange("(c p j) (g n) -> c g p j n", p=P, j=4, g=2),
+        }
+        b_view = w_share_bytes.rearrange("(c p j) (g n) -> c g p j n", p=P, j=4, g=2)
+
+        k_raw, w_raw, b_raw = {}, {}, {}
+        wide, w_grp, k_grp = {}, {}, {}
+        codes, scales = {}, {}
+        banks, silu, h_grp = {}, {}, {}
+
+        def load_k(x, c, h):
+            t = keep.tile([P, 4, 512], BF16, name=f"k_{x}{c}{h}")
+            k_raw[x, c, h] = t
+            nc.sync.dma_start(out=t[:], in_=k_view[x][h, c])
+
+        def load_w(w, c, g):
+            t = wrawp.tile([P, 4, 512], BF16, name="wraw", tag="wraw")
+            w_raw[w, c, g] = t
+            nc.sync.dma_start(out=t[:], in_=w_view[w][c, g])
+
+        def load_b(c, g):
+            t = keep.tile([P, 4, 512], U8, name=f"bytes{c}{g}")
+            b_raw[c, g] = t
+            nc.sync.dma_start(out=t[:], in_=b_view[c, g])
+
+        scale_sb = keep.tile([P, 2, 4], F32, name="scale_sb")
+        nc.scalar.dma_start(out=scale_sb[:], in_=w_share_scale.rearrange("(c p j) o -> p c (j o)", p=P, j=4))
+        gain_sb = keep.tile([P, 2, 4], BF16, name="gain_sb")
+        nc.scalar.dma_start(out=gain_sb[:], in_=g_hid.rearrange("(g p t) -> p g t", p=P, t=4))
+        warm = keep.tile([P, 1], F32, name="warm")
+        nc.gpsimd.memset(warm[:], 0.0)
+        warm2 = keep.tile([P, 1], F32, name="warm2")
+        nc.scalar.activation(out=warm2[:], in_=warm[:], func=ACT.Silu)
+        ident = keep.tile([P, P], F32, name="ident")
+        make_identity(nc, ident[:])
+        ident_bf = keep.tile([P, P], BF16, name="ident_bf")
+        nc.gpsimd.tensor_copy(out=ident_bf[:], in_=ident[:])
+
+        def transposes(x, c, h):
+            words = k_raw[x, c, h][:].bitcast(F32)
+            for i in range(2):
+                bank = psum.tile([P, 2, 2, P], F32, name="bank", tag="bank")
+                banks["t", x, c, h, i] = bank
+                for b in range(2):
+                    for u in range(2):
+                        nc.tensor.transpose(bank[:, b, u, :], words[:, 2 * i + b, u:256:2], ident[:])
+
+        def move(engine, dst, src):
+            if engine == "S":
+                nc.scalar.copy(dst, src)
+            else:
+                nc.vector.tensor_copy(dst, src)
+
+        def empty_transposed(x, c, h, i, engine="S"):
+            if i == 0:
+                k_grp[x, c, h] = kgrpp.tile([P, 2048], BF16, name="kgrp", tag="kgrp", align_bytes=64)
+            dst = k_grp[x, c, h][:].bitcast(F32).rearrange("p (i b r u) -> p i b r u", i=2, b=2, u=2)
+            move(engine, dst[:, i], banks["t", x, c, h, i][:].rearrange("p b u r -> p b r u"))
+
+        def quantize(key, src):
+            cd = keep.tile([P, 512], U32, name="cd_" + "_".join(str(v) for v in key), align_bytes=64)
+            sc = keep.tile([P, 512], U8, name="sc_" + "_".join(str(v) for v in key), align_bytes=64)
+            codes[key], scales[key] = cd, sc
+            nc.vector.quantize_mx(out=cd[:].bitcast(FP8X4), scales=sc[:], in_=src[:])
+
+        def quant_k(x, c, h):
+            quantize(("k", x, c, h), k_grp[x, c, h])
+
+        def widen(c, g):
+            t = widep.tile([P, 4, 512], BF16, name="wide", tag="wide")
+            wide[c, g] = t
+            for j in range(4):
+                nc.scalar.activation(
+                    out=t[:, j, :],
+                    in_=b_raw[c, g][:, j, :].bitcast(FP8),
+                    func=ACT.Copy,
+                    scale=scale_sb[:, c, j : j + 1],
+                )
+
+        def interleaved(w, c, g):
+            src = wide[c, g] if w == "s" else w_raw[w, c, g]
+            if w in "rs":
+                return src[:].rearrange("p j (m t) -> p t m j", t=4)
+            return src[:].rearrange("p j (t m) -> p t m j", t=4)
+
+        def w_grp_tile(w, c, g):
+            w_grp[w, c, g] = wgrpp.tile([P, 2048], BF16, name="wgrp", tag="wgrp", align_bytes=64)
+            return w_grp[w, c, g]
+
+        def interleave(w, c, g, engine="V"):
+            t = w_grp_tile(w, c, g)
+            if w in "rs":
+                move(engine, t[:].rearrange("p (t m j) -> p t m j", t=4, j=4), interleaved(w, c, g))
+            else:
+                dst = t[:].rearrange("p (c i j) -> p c j i", i=4, j=4)
+                move(engine, dst, w_raw[w, c, g][:].rearrange("p j (c i) -> p c j i", i=4))
+
+        def interleave_pe(w, c, g):
+            view = interleaved(w, c, g)
+            for half in range(2):
+                bank = psum.tile([P, 2, P, 4], BF16, name="bank", tag="bank")
+                banks["i", w, c, g, half] = bank
+                for q in range(2):
+                    nc.tensor.matmul(
+                        bank[:, q], lhsT=ident_bf[:], rhs=view[:, 2 * half + q], start=True, stop=True
+                    )
+
+        def empty_interleaved(w, c, g, engine="S"):
+            t = w_grp_tile(w, c, g)
+            for half in range(2):
+                bank = banks["i", w, c, g, half][:].rearrange("p q m j -> p (q m j)")
+                move(engine, t[:, half * 1024 : (half + 1) * 1024], bank)
+
+        def quant_w(w, c, g):
+            quantize(("w", w, c, g), w_grp[w, c, g])
+
+        def mm(g, h, x, c):
+            first, last = (x, c) == ("r", 0), (x, c) == ("s", 1)
+            for t in range(4):
+                if first:
+                    banks["u", g, h, t] = psum.tile([P, 512], F32, name="bank", tag="bank")
+                cols = slice(t * P, (t + 1) * P)
+                nc.tensor.matmul_mx(
+                    out=banks["u", g, h, t][:],
+                    lhsT=codes["w", x, c, g][:, cols].bitcast(FP8X4),
+                    lhsT_scale=scales["w", x, c, g][:, cols],
+                    rhs=codes["k", x, c, h][:].bitcast(FP8X4),
+                    rhs_scale=scales["k", x, c, h][:],
+                    start=first,
+                    stop=last,
+                )
+
+        def act_silu(g, h):
+            t = hidp.tile([P, 4, 512], F32, name="silu", tag="silu")
+            silu[g, h] = t
+            for i in range(4):
+                nc.scalar.activation(out=t[:, i, :], in_=banks["u", g, h, i][:], func=ACT.Silu)
+
+        def gain(g, h):
+            t = hidp.tile([P, 2048], BF16, name="hgrp", tag="hgrp", align_bytes=64)
+            h_grp[g, h] = t
+            nc.vector.tensor_tensor(
+                out=t[:].rearrange("p (n t) -> p n t", t=4),
+                in0=silu[g, h][:].rearrange("p t n -> p n t"),
+                in1=gain_sb[:, g : g + 1, :].to_broadcast([P, 512, 4]),
+                op=ALU.mult,
+            )
+
+        def quant_h(g, h):
+            quantize(("h", g, h), h_grp[g, h])
+
+        def mm2(h, d, b):
+            cols = slice(b * P, (b + 1) * P)
+            for w in "gd":
+                bank = psum.tile([P, 512], F32, name="bank", tag="bank")
+                banks[w, h, d, b] = bank
+                for c in range(2):
+                    nc.tensor.matmul_mx(
+                        out=bank[:],
+                        lhsT=codes["h", c, h][:, cols].bitcast(FP8X4),
+                        lhsT_scale=scales["h", c, h][:, cols],
+                        rhs=codes["w", w, c, d][:].bitcast(FP8X4),
+                        rhs_scale=scales["w", w, c, d][:],
+                        start=(c == 0),
+                        stop=(c == 1),
+                    )
+
+        gates, prods = {}, {}
+
+        def act_gate(h, d, b):
+            t = outp.tile([P, 512], F32, name="gate", tag="gate")
+            gates[h, d, b] = t
+            nc.scalar.activation(out=t[:], in_=banks["g", h, d, b][:], func=ACT.Sigmoid)
+
+        def product(h, d, b):
+            t = outp.tile([P, 512], F32, name="prod", tag="prod")
+            prods[h, d, b] = t
+            nc.vector.tensor_tensor(out=t[:], in0=banks["d", h, d, b][:], in1=gates[h, d, b][:], op=ALU.mult)
+
+        def residual(h, d, b, engine):
+            t = outp.tile([P, 512], F32, name="res", tag="res")
+            engine.tensor_tensor(out=t[:], in0=prods[h, d, b][:], in1=k_raw["r", d, h][:, b, :], op=ALU.add)
+            r0 = h * 512 + b * P
+            nc.sync.dma_start(out=out[r0 : r0 + P, d * 512 : (d + 1) * 512], in_=t[:])
+
+        PASSES = (("r", 0), ("s", 0), ("r", 1), ("s", 1))
+        ROUTE = {"d00":"PS","d10":"V","g00":"V","g10":"PS","d01":"S","d11":"PS","g01":"V","g11":"PV"}
+        ON_G = [(h, d, b) for h in range(2) for d in range(2) for b in (0, 2)]
+
+        def weights(w, c, g):
+            r = ROUTE[w + str(c) + str(g)]
+            if r[0] == "P":
+                interleave_pe(w, c, g)
+                empty_interleaved(w, c, g, r[1])
+            else:
+                interleave(w, c, g, r)
+        load_w("r", 0, 0)
+        load_b(0, 0)
+        load_k("r", 0, 0)
+        load_w("r", 1, 0)
+        load_b(1, 0)
+        load_k("s", 0, 0)
+        load_k("r", 1, 0)
+        load_k("s", 1, 0)
+        for x in "rs":
+            for c in range(2):
+                load_k(x, c, 1)
+        load_w("r", 0, 1)
+        load_w("r", 1, 1)
+        load_b(0, 1)
+        load_b(1, 1)
+        load_w("d", 0, 0)
+        load_w("g", 0, 0)
+        load_w("d", 1, 0)
+
+        def empty_k(x, c, h):
+            for i in range(2):
+                empty_transposed(x, c, h, i)
+
+        interleave("r", 0, 0)
+        widen(0, 0)
+        transposes("r", 0, 0)
+        empty_k("r", 0, 0)
+        quant_w("r", 0, 0)
+        interleave("r", 1, 0)
+        quant_k("r", 0, 0)
+        transposes("s", 0, 0)
+        interleave("s", 0, 0)
+        quant_w("r", 1, 0)
+        mm(0, 0, "r", 0)
+        widen(1, 0)
+        transposes("r", 1, 0)
+        empty_k("s", 0, 0)
+        empty_k("r", 1, 0)
+        quant_w("s", 0, 0)
+        quant_k("s", 0, 0)
+        interleave("s", 1, 0)
+        quant_k("r", 1, 0)
+        mm(0, 0, "s", 0)
+        mm(0, 0, "r", 1)
+        transposes("s", 1, 0)
+        empty_k("s", 1, 0)
+        quant_w("s", 1, 0)
+        quant_k("s", 1, 0)
+        mm(0, 0, "s", 1)
+        transposes("r", 0, 1)
+        transposes("r", 1, 1)
+        empty_k("r", 0, 1)
+        empty_k("r", 1, 1)
+        interleave("r", 0, 1)
+        load_w("g", 1, 0)
+        for w, c in (("d", 0), ("g", 0), ("d", 1), ("g", 1)):
+            load_w(w, c, 1)
+        quant_k("r", 0, 1)
+        quant_w("r", 0, 1)
+        quant_k("r", 1, 1)
+        act_silu(0, 0)
+        transposes("s", 0, 1)
+        transposes("s", 1, 1)
+        empty_k("s", 0, 1)
+        empty_k("s", 1, 1)
+        interleave("r", 1, 1)
+        gain(0, 0)
+        quant_w("r", 1, 1)
+        quant_k("s", 0, 1)
+        quant_k("s", 1, 1)
+        quant_h(0, 0)
+        for x, c in PASSES:
+            mm(0, 1, x, c)
+        widen(0, 1)
+        widen(1, 1)
+        interleave("s", 0, 1)
+        act_silu(0, 1)
+        interleave("s", 1, 1)
+        quant_w("s", 0, 1)
+        quant_w("s", 1, 1)
+        for x, c in PASSES:
+            mm(1, 0, x, c)
+        weights("d", 0, 0)
+        gain(0, 1)
+        weights("d", 1, 0)
+        quant_h(0, 1)
+        act_silu(1, 0)
+        for x, c in PASSES:
+            mm(1, 1, x, c)
+        quant_w("d", 0, 0)
+        weights("g", 0, 0)
+        quant_w("d", 1, 0)
+        weights("g", 1, 0)
+        gain(1, 0)
+        quant_w("g", 0, 0)
+        quant_h(1, 0)
+        quant_w("g", 1, 0)
+        act_silu(1, 1)
+        weights("d", 0, 1)
+        weights("d", 1, 1)
+        gain(1, 1)
+        quant_h(1, 1)
+        tail = []
+
+        def stage2(h, d, b):
+            mm2(h, d, b)
+            act_gate(h, d, b)
+            tail.append((h, d, b))
+
+        def finish(n):
+            while len(tail) > n:
+                product(*tail[0])
+                residual(*tail[0], nc.gpsimd if tail[0] in ON_G else nc.vector)
+                tail.remove(tail[0])
+
+        for b in range(4):
+            stage2(0, 0, b)
+            finish(1)
+            if b == 1:
+                quant_w("d", 0, 1)
+                quant_w("d", 1, 1)
+                weights("g", 0, 1)
+                weights("g", 1, 1)
+        for b in range(4):
+            stage2(1, 0, b)
+            finish(1)
+            if b == 1:
+                quant_w("g", 0, 1)
+                quant_w("g", 1, 1)
+        for h in range(2):
+            for b in range(4):
+                stage2(h, 1, b)
+                finish(1)
+        finish(0)

@@ -72,8 +72,6 @@ def tile_cachetocachegatedkeyfuser_kernel(
         nc.scalar.activation(out=warm2[:], in_=warm[:], func=ACT.Silu)
         ident = keep.tile([P, P], F32, name="ident")
         make_identity(nc, ident[:])
-        ident_bf = keep.tile([P, P], BF16, name="ident_bf")
-        nc.gpsimd.tensor_copy(out=ident_bf[:], in_=ident[:])
 
         def transposes(x, c, h):
             words = k_raw[x, c, h][:].bitcast(F32)
@@ -84,17 +82,16 @@ def tile_cachetocachegatedkeyfuser_kernel(
                     for u in range(2):
                         nc.tensor.transpose(bank[:, b, u, :], words[:, 2 * i + b, u:256:2], ident[:])
 
-        def move(engine, dst, src):
-            if engine == "S":
-                nc.scalar.copy(dst, src)
-            else:
-                nc.vector.tensor_copy(dst, src)
-
-        def empty_transposed(x, c, h, i, engine="S"):
-            if i == 0:
-                k_grp[x, c, h] = kgrpp.tile([P, 2048], BF16, name="kgrp", tag="kgrp", align_bytes=64)
-            dst = k_grp[x, c, h][:].bitcast(F32).rearrange("p (i b r u) -> p i b r u", i=2, b=2, u=2)
-            move(engine, dst[:, i], banks["t", x, c, h, i][:].rearrange("p b u r -> p b r u"))
+        def empty_transposed(x, c, h, engines):
+            g = kgrpp.tile([P, 2048], BF16, name="kgrp", tag="kgrp", align_bytes=64)
+            k_grp[x, c, h] = g
+            dst = g[:].bitcast(F32).rearrange("p (i b r u) -> p i b r u", i=2, b=2, u=2)
+            for i in range(2):
+                src = banks["t", x, c, h, i][:].rearrange("p b u r -> p b r u")
+                if engines[i] == "S":
+                    nc.scalar.copy(dst[:, i], src)
+                else:
+                    nc.vector.tensor_copy(dst[:, i], src)
 
         def quantize(key, src):
             cd = keep.tile([P, 512], U32, name="cd_" + "_".join(str(v) for v in key), align_bytes=64)
@@ -116,71 +113,56 @@ def tile_cachetocachegatedkeyfuser_kernel(
                     scale=scale_sb[:, c, j : j + 1],
                 )
 
-        def interleaved(w, c, g):
+        def interleave(w, c, g, engine="V"):
+            t = wgrpp.tile([P, 2048], BF16, name="wgrp", tag="wgrp", align_bytes=64)
+            w_grp[w, c, g] = t
             src = wide[c, g] if w == "s" else w_raw[w, c, g]
             if w in "rs":
-                return src[:].rearrange("p j (m t) -> p t m j", t=4)
-            return src[:].rearrange("p j (t m) -> p t m j", t=4)
-
-        def w_grp_tile(w, c, g):
-            w_grp[w, c, g] = wgrpp.tile([P, 2048], BF16, name="wgrp", tag="wgrp", align_bytes=64)
-            return w_grp[w, c, g]
-
-        def interleave(w, c, g, engine="V"):
-            t = w_grp_tile(w, c, g)
-            if w in "rs":
-                move(engine, t[:].rearrange("p (t m j) -> p t m j", t=4, j=4), interleaved(w, c, g))
+                dst = t[:].rearrange("p (t m j) -> p t m j", t=4, j=4)
+                view = src[:].rearrange("p j (m t) -> p t m j", t=4)
             else:
                 dst = t[:].rearrange("p (c i j) -> p c j i", i=4, j=4)
-                move(engine, dst, w_raw[w, c, g][:].rearrange("p j (c i) -> p c j i", i=4))
-
-        def interleave_pe(w, c, g):
-            view = interleaved(w, c, g)
-            for half in range(2):
-                bank = psum.tile([P, 2, P, 4], BF16, name="bank", tag="bank")
-                banks["i", w, c, g, half] = bank
-                for q in range(2):
-                    nc.tensor.matmul(
-                        bank[:, q], lhsT=ident_bf[:], rhs=view[:, 2 * half + q], start=True, stop=True
-                    )
-
-        def empty_interleaved(w, c, g, engine="S"):
-            t = w_grp_tile(w, c, g)
-            for half in range(2):
-                bank = banks["i", w, c, g, half][:].rearrange("p q m j -> p (q m j)")
-                move(engine, t[:, half * 1024 : (half + 1) * 1024], bank)
+                view = src[:].rearrange("p j (c i) -> p c j i", i=4)
+            if engine == "V":
+                nc.vector.tensor_copy(dst, view)
+            else:
+                nc.scalar.copy(dst, view)
 
         def quant_w(w, c, g):
             quantize(("w", w, c, g), w_grp[w, c, g])
 
-        def mm(g, h, x, c):
-            first, last = (x, c) == ("r", 0), (x, c) == ("s", 1)
+        def mm(g, h, b):
+            bank = psum.tile([P, 4, P], F32, name="bank", tag="bank")
+            banks["u", g, h, b] = bank
+            tokens = slice(b * P, (b + 1) * P)
             for t in range(4):
-                if first:
-                    banks["u", g, h, t] = psum.tile([P, 512], F32, name="bank", tag="bank")
                 cols = slice(t * P, (t + 1) * P)
-                nc.tensor.matmul_mx(
-                    out=banks["u", g, h, t][:],
-                    lhsT=codes["w", x, c, g][:, cols].bitcast(FP8X4),
-                    lhsT_scale=scales["w", x, c, g][:, cols],
-                    rhs=codes["k", x, c, h][:].bitcast(FP8X4),
-                    rhs_scale=scales["k", x, c, h][:],
-                    start=first,
-                    stop=last,
-                )
+                for x, c in PASSES:
+                    nc.tensor.matmul_mx(
+                        out=bank[:, t],
+                        lhsT=codes["w", x, c, g][:, cols].bitcast(FP8X4),
+                        lhsT_scale=scales["w", x, c, g][:, cols],
+                        rhs=codes["k", x, c, h][:, tokens].bitcast(FP8X4),
+                        rhs_scale=scales["k", x, c, h][:, tokens],
+                        start=(x, c) == PASSES[0],
+                        stop=(x, c) == PASSES[-1],
+                    )
 
-        def act_silu(g, h):
-            t = hidp.tile([P, 4, 512], F32, name="silu", tag="silu")
-            silu[g, h] = t
-            for i in range(4):
-                nc.scalar.activation(out=t[:, i, :], in_=banks["u", g, h, i][:], func=ACT.Silu)
+        def act_silu(g, h, b):
+            if b == 0:
+                silu[g, h] = hidp.tile([P, 512, 4], F32, name="silu", tag="silu")
+            nc.scalar.activation(
+                out=silu[g, h][:, b * P : (b + 1) * P, :],
+                in_=banks["u", g, h, b][:].rearrange("p t n -> p n t"),
+                func=ACT.Silu,
+            )
 
         def gain(g, h):
             t = hidp.tile([P, 2048], BF16, name="hgrp", tag="hgrp", align_bytes=64)
             h_grp[g, h] = t
             nc.vector.tensor_tensor(
                 out=t[:].rearrange("p (n t) -> p n t", t=4),
-                in0=silu[g, h][:].rearrange("p t n -> p n t"),
+                in0=silu[g, h][:],
                 in1=gain_sb[:, g : g + 1, :].to_broadcast([P, 512, 4]),
                 op=ALU.mult,
             )
@@ -209,132 +191,111 @@ def tile_cachetocachegatedkeyfuser_kernel(
         def act_gate(h, d, b):
             t = outp.tile([P, 512], F32, name="gate", tag="gate")
             gates[h, d, b] = t
-            nc.scalar.activation(out=t[:], in_=banks["g", h, d, b][:], func=ACT.Sigmoid)
+            nc.scalar.activation(out=t[:], in_=banks["g", h, d, b][:], func=ACT.Tanh, scale=0.5)
 
         def product(h, d, b):
             t = outp.tile([P, 512], F32, name="prod", tag="prod")
             prods[h, d, b] = t
-            nc.vector.tensor_tensor(out=t[:], in0=banks["d", h, d, b][:], in1=gates[h, d, b][:], op=ALU.mult)
+            nc.vector.scalar_tensor_tensor(
+                out=t[:], in0=gates[h, d, b][:], scalar=1.0, in1=banks["d", h, d, b][:], op0=ALU.add, op1=ALU.mult
+            )
 
-        def residual(h, d, b, engine):
+        def residual(h, d, b):
             t = outp.tile([P, 512], F32, name="res", tag="res")
-            engine.tensor_tensor(out=t[:], in0=prods[h, d, b][:], in1=k_raw["r", d, h][:, b, :], op=ALU.add)
+            nc.vector.scalar_tensor_tensor(
+                out=t[:], in0=prods[h, d, b][:], scalar=0.5, in1=k_raw["r", d, h][:, b, :], op0=ALU.mult, op1=ALU.add
+            )
             r0 = h * 512 + b * P
             nc.sync.dma_start(out=out[r0 : r0 + P, d * 512 : (d + 1) * 512], in_=t[:])
 
         PASSES = (("r", 0), ("s", 0), ("r", 1), ("s", 1))
-        ROUTE = {"d00":"PS","d10":"V","g00":"V","g10":"PS","d01":"S","d11":"PS","g01":"V","g11":"PV"}
-        ON_G = [(h, d, b) for h in range(2) for d in range(2) for b in (0, 2)]
 
-        def weights(w, c, g):
-            r = ROUTE[w + str(c) + str(g)]
-            if r[0] == "P":
-                interleave_pe(w, c, g)
-                empty_interleaved(w, c, g, r[1])
-            else:
-                interleave(w, c, g, r)
-        load_w("r", 0, 0)
+        def unit(g, h):
+            for b in range(4):
+                mm(g, h, b)
+                act_silu(g, h, b)
+
         load_b(0, 0)
+        load_w("r", 0, 0)
         load_k("r", 0, 0)
-        load_w("r", 1, 0)
         load_b(1, 0)
+        load_w("r", 1, 0)
         load_k("s", 0, 0)
         load_k("r", 1, 0)
         load_k("s", 1, 0)
+        load_b(0, 1)
+        load_b(1, 1)
+        load_w("r", 0, 1)
+        load_w("r", 1, 1)
         for x in "rs":
             for c in range(2):
                 load_k(x, c, 1)
-        load_w("r", 0, 1)
-        load_w("r", 1, 1)
-        load_b(0, 1)
-        load_b(1, 1)
         load_w("d", 0, 0)
         load_w("g", 0, 0)
         load_w("d", 1, 0)
 
-        def empty_k(x, c, h):
-            for i in range(2):
-                empty_transposed(x, c, h, i)
-
-        interleave("r", 0, 0)
         widen(0, 0)
+        interleave("r", 0, 0)
         transposes("r", 0, 0)
-        empty_k("r", 0, 0)
+        empty_transposed("r", 0, 0, "SS")
+        interleave("s", 0, 0)
         quant_w("r", 0, 0)
+        quant_w("s", 0, 0)
+        widen(1, 0)
         interleave("r", 1, 0)
         quant_k("r", 0, 0)
         transposes("s", 0, 0)
-        interleave("s", 0, 0)
-        quant_w("r", 1, 0)
-        mm(0, 0, "r", 0)
-        widen(1, 0)
-        transposes("r", 1, 0)
-        empty_k("s", 0, 0)
-        empty_k("r", 1, 0)
-        quant_w("s", 0, 0)
-        quant_k("s", 0, 0)
+        empty_transposed("s", 0, 0, "SS")
         interleave("s", 1, 0)
-        quant_k("r", 1, 0)
-        mm(0, 0, "s", 0)
-        mm(0, 0, "r", 1)
-        transposes("s", 1, 0)
-        empty_k("s", 1, 0)
+        quant_w("r", 1, 0)
+        quant_k("s", 0, 0)
+        transposes("r", 1, 0)
+        empty_transposed("r", 1, 0, "SS")
         quant_w("s", 1, 0)
-        quant_k("s", 1, 0)
-        mm(0, 0, "s", 1)
-        transposes("r", 0, 1)
-        transposes("r", 1, 1)
-        empty_k("r", 0, 1)
-        empty_k("r", 1, 1)
+        transposes("s", 1, 0)
+        quant_k("r", 1, 0)
+        empty_transposed("s", 1, 0, "SS")
         interleave("r", 0, 1)
+        quant_k("s", 1, 0)
+        unit(0, 0)
+        widen(0, 1)
+        interleave("r", 1, 1)
+        quant_w("r", 0, 1)
         load_w("g", 1, 0)
         for w, c in (("d", 0), ("g", 0), ("d", 1), ("g", 1)):
             load_w(w, c, 1)
-        quant_k("r", 0, 1)
-        quant_w("r", 0, 1)
-        quant_k("r", 1, 1)
-        act_silu(0, 0)
-        transposes("s", 0, 1)
-        transposes("s", 1, 1)
-        empty_k("s", 0, 1)
-        empty_k("s", 1, 1)
-        interleave("r", 1, 1)
-        gain(0, 0)
-        quant_w("r", 1, 1)
-        quant_k("s", 0, 1)
-        quant_k("s", 1, 1)
-        quant_h(0, 0)
-        for x, c in PASSES:
-            mm(0, 1, x, c)
-        widen(0, 1)
+        transposes("r", 0, 1)
+        transposes("r", 1, 1)
         widen(1, 1)
+        quant_w("r", 1, 1)
         interleave("s", 0, 1)
-        act_silu(0, 1)
         interleave("s", 1, 1)
         quant_w("s", 0, 1)
         quant_w("s", 1, 1)
-        for x, c in PASSES:
-            mm(1, 0, x, c)
-        weights("d", 0, 0)
-        gain(0, 1)
-        weights("d", 1, 0)
-        quant_h(0, 1)
-        act_silu(1, 0)
-        for x, c in PASSES:
-            mm(1, 1, x, c)
-        quant_w("d", 0, 0)
-        weights("g", 0, 0)
-        quant_w("d", 1, 0)
-        weights("g", 1, 0)
+        unit(1, 0)
+        empty_transposed("r", 0, 1, "SS")
+        gain(0, 0)
+        quant_h(0, 0)
+        empty_transposed("r", 1, 1, "SS")
+        transposes("s", 0, 1)
+        transposes("s", 1, 1)
+        quant_k("r", 0, 1)
+        quant_k("r", 1, 1)
+        interleave("g", 0, 0, "V")
+        empty_transposed("s", 0, 1, "SS")
+        empty_transposed("s", 1, 1, "SS")
         gain(1, 0)
+        interleave("d", 0, 0, "S")
         quant_w("g", 0, 0)
+        quant_k("s", 0, 1)
+        quant_k("s", 1, 1)
+        unit(0, 1)
         quant_h(1, 0)
+        interleave("d", 1, 0, "S")
+        interleave("g", 1, 0, "S")
+        quant_w("d", 0, 0)
         quant_w("g", 1, 0)
-        act_silu(1, 1)
-        weights("d", 0, 1)
-        weights("d", 1, 1)
-        gain(1, 1)
-        quant_h(1, 1)
+        quant_w("d", 1, 0)
         tail = []
 
         def stage2(h, d, b):
@@ -345,25 +306,29 @@ def tile_cachetocachegatedkeyfuser_kernel(
         def finish(n):
             while len(tail) > n:
                 product(*tail[0])
-                residual(*tail[0], nc.gpsimd if tail[0] in ON_G else nc.vector)
+                residual(*tail[0])
                 tail.remove(tail[0])
 
         for b in range(4):
             stage2(0, 0, b)
             finish(1)
+            if b == 0:
+                gain(0, 1)
+                interleave("d", 0, 1, "S")
             if b == 1:
+                quant_h(0, 1)
                 quant_w("d", 0, 1)
-                quant_w("d", 1, 1)
-                weights("g", 0, 1)
-                weights("g", 1, 1)
-        for b in range(4):
-            stage2(1, 0, b)
-            finish(1)
-            if b == 1:
-                quant_w("g", 0, 1)
-                quant_w("g", 1, 1)
-        for h in range(2):
+        unit(1, 1)
+        interleave("g", 0, 1, "S")
+        interleave("d", 1, 1, "S")
+        quant_w("g", 0, 1)
+        interleave("g", 1, 1, "V")
+        quant_w("d", 1, 1)
+        quant_w("g", 1, 1)
+        gain(1, 1)
+        quant_h(1, 1)
+        for h, d in ((0, 1), (1, 0), (1, 1)):
             for b in range(4):
-                stage2(h, 1, b)
+                stage2(h, d, b)
                 finish(1)
         finish(0)

@@ -23,44 +23,56 @@ def tile_cachetocachegatedkeyfuser_kernel(
     nc = tc.nc
     with ExitStack() as ctx:
         keep = ctx.enter_context(tc.tile_pool(name="keep", bufs=1))
-        wrawp = ctx.enter_context(tc.tile_pool(name="wrawp", bufs=7))
-        widep = ctx.enter_context(tc.tile_pool(name="widep", bufs=3))
-        wgrpp = ctx.enter_context(tc.tile_pool(name="wgrpp", bufs=4))
-        kgrpp = ctx.enter_context(tc.tile_pool(name="kgrpp", bufs=3))
+        rawp = ctx.enter_context(tc.tile_pool(name="rawp", bufs=8))
+        grpp = ctx.enter_context(tc.tile_pool(name="grpp", bufs=9))
         hidp = ctx.enter_context(tc.tile_pool(name="hidp", bufs=2))
-        outp = ctx.enter_context(tc.tile_pool(name="outp", bufs=4))
+        outp = ctx.enter_context(tc.tile_pool(name="outp", bufs=3))
+        resp = ctx.enter_context(tc.tile_pool(name="resp", bufs=5))
         psum = ctx.enter_context(tc.psum_pool(name="psum", bufs=8))
 
+        ctx.enter_context(tc.manual_schedule())
         k_view = {
-            "r": k_recv.rearrange("(h b r) (c k) -> h c r b k", b=4, r=P, c=2),
-            "s": k_share.rearrange("(h b r) (c k) -> h c r b k", b=4, r=P, c=2),
+            "r": k_recv.rearrange("(h i b r) k -> h i r b k", h=2, i=2, r=P),
+            "s": k_share.rearrange("(h i b r) k -> h i r b k", h=2, i=2, r=P),
         }
         w_view = {
             "r": w_recv.rearrange("(c p j) (g n) -> c g p j n", p=P, j=4, g=2),
-            "d": w_delta.rearrange("(c p j) (g n) -> c g p j n", p=P, j=4, g=2),
-            "g": w_gate.rearrange("(c p j) (g n) -> c g p j n", p=P, j=4, g=2),
+            "d": w_delta.rearrange("(c p j) n -> c p j n", p=P, j=4),
+            "g": w_gate.rearrange("(c p j) n -> c p j n", p=P, j=4),
         }
-        b_view = w_share_bytes.rearrange("(c p j) (g n) -> c g p j n", p=P, j=4, g=2)
+        b_view = w_share_bytes.rearrange("(c p j) n -> c p j n", p=P, j=4)
 
         k_raw, w_raw, b_raw = {}, {}, {}
         wide, w_grp, k_grp = {}, {}, {}
         codes, scales = {}, {}
         banks, silu, h_grp = {}, {}, {}
+        gates, prods = {}, {}
 
-        def load_k(x, c, h):
-            t = keep.tile([P, 4, 512], BF16, name=f"k_{x}{c}{h}")
-            k_raw[x, c, h] = t
-            nc.sync.dma_start(out=t[:], in_=k_view[x][h, c])
-
-        def load_w(w, c, g):
-            t = wrawp.tile([P, 4, 512], BF16, name="wraw", tag="wraw")
-            w_raw[w, c, g] = t
-            nc.sync.dma_start(out=t[:], in_=w_view[w][c, g])
-
-        def load_b(c, g):
-            t = keep.tile([P, 4, 512], U8, name=f"bytes{c}{g}")
-            b_raw[c, g] = t
-            nc.sync.dma_start(out=t[:], in_=b_view[c, g])
+        def load(n):
+            if n[0] == "K":
+                x, h, i = n[1], int(n[2]), int(n[3])
+                if x == "r":
+                    t = keep.tile([P, 2, 1024], BF16, name="k_" + n)
+                else:
+                    t = rawp.tile([P, 4, 512], BF16, name="raw", tag="raw")
+                    t = t[:].rearrange("p a b -> p (a b)").rearrange("p (b k) -> p b k", b=2)
+                k_raw[x, h, i] = t
+                nc.sync.dma_start(out=t[:], in_=k_view[x][h, i])
+            elif n[0] == "B":
+                t = keep.tile([P, 4, 1024], U8, name="bytes" + n[1])
+                b_raw[int(n[1])] = t
+                nc.sync.dma_start(out=t[:], in_=b_view[int(n[1])])
+            elif n[1] == "r":
+                c, g = int(n[2]), int(n[3])
+                t = rawp.tile([P, 4, 512], BF16, name="raw", tag="raw")
+                w_raw["r", c, g] = t[:]
+                nc.sync.dma_start(out=t[:], in_=w_view["r"][c, g])
+            else:
+                c = int(n[2])
+                t = keep.tile([P, 4, 1024], BF16, name="w_" + n)
+                for g in range(2):
+                    w_raw[n[1], c, g] = t[:, :, g * 512 : (g + 1) * 512]
+                nc.sync.dma_start(out=t[:], in_=w_view[n[1]][c])
 
         scale_sb = keep.tile([P, 2, 4], F32, name="scale_sb")
         nc.scalar.dma_start(out=scale_sb[:], in_=w_share_scale.rearrange("(c p j) o -> p c (j o)", p=P, j=4))
@@ -72,26 +84,28 @@ def tile_cachetocachegatedkeyfuser_kernel(
         nc.scalar.activation(out=warm2[:], in_=warm[:], func=ACT.Silu)
         ident = keep.tile([P, P], F32, name="ident")
         make_identity(nc, ident[:])
+        ident_bf = keep.tile([P, P], BF16, name="ident_bf")
+        nc.gpsimd.tensor_copy(out=ident_bf[:], in_=ident[:])
 
-        def transposes(x, c, h):
-            words = k_raw[x, c, h][:].bitcast(F32)
-            for i in range(2):
-                bank = psum.tile([P, 2, 2, P], F32, name="bank", tag="bank")
-                banks["t", x, c, h, i] = bank
-                for b in range(2):
-                    for u in range(2):
-                        nc.tensor.transpose(bank[:, b, u, :], words[:, 2 * i + b, u:256:2], ident[:])
+        def move(engine, dst, src):
+            if engine == "S":
+                nc.scalar.copy(dst, src)
+            else:
+                nc.vector.tensor_copy(dst, src)
 
-        def empty_transposed(x, c, h, engines):
-            g = kgrpp.tile([P, 2048], BF16, name="kgrp", tag="kgrp", align_bytes=64)
-            k_grp[x, c, h] = g
-            dst = g[:].bitcast(F32).rearrange("p (i b r u) -> p i b r u", i=2, b=2, u=2)
-            for i in range(2):
-                src = banks["t", x, c, h, i][:].rearrange("p b u r -> p b r u")
-                if engines[i] == "S":
-                    nc.scalar.copy(dst[:, i], src)
-                else:
-                    nc.vector.tensor_copy(dst[:, i], src)
+        def transposes(x, c, h, i):
+            words = k_raw[x, h, i][:].bitcast(F32)
+            bank = psum.tile([P, 2, 2, P], F32, name="bank", tag="bank")
+            banks["t", x, c, h, i] = bank
+            for b in range(2):
+                for u in range(2):
+                    nc.tensor.transpose(bank[:, b, u, :], words[:, b, c * 256 + u : (c + 1) * 256 : 2], ident[:])
+
+        def empty_transposed(x, c, h, i, engine):
+            if (x, c, h) not in k_grp:
+                k_grp[x, c, h] = grpp.tile([P, 2048], BF16, name="grp", tag="grp", align_bytes=64)
+            dst = k_grp[x, c, h][:].bitcast(F32).rearrange("p (i b r u) -> p i b r u", i=2, b=2, u=2)
+            move(engine, dst[:, i], banks["t", x, c, h, i][:].rearrange("p b u r -> p b r u"))
 
         def quantize(key, src):
             cd = keep.tile([P, 512], U32, name="cd_" + "_".join(str(v) for v in key), align_bytes=64)
@@ -102,31 +116,44 @@ def tile_cachetocachegatedkeyfuser_kernel(
         def quant_k(x, c, h):
             quantize(("k", x, c, h), k_grp[x, c, h])
 
-        def widen(c, g):
-            t = widep.tile([P, 4, 512], BF16, name="wide", tag="wide")
-            wide[c, g] = t
-            for j in range(4):
+        def widen(c, g, half):
+            if (c, g) not in wide:
+                wide[c, g] = rawp.tile([P, 4, 512], BF16, name="raw", tag="raw")
+            for j in (2 * half, 2 * half + 1):
                 nc.scalar.activation(
-                    out=t[:, j, :],
-                    in_=b_raw[c, g][:, j, :].bitcast(FP8),
+                    out=wide[c, g][:, j, :],
+                    in_=b_raw[c][:, j, g * 512 : (g + 1) * 512].bitcast(FP8),
                     func=ACT.Copy,
                     scale=scale_sb[:, c, j : j + 1],
                 )
 
-        def interleave(w, c, g, engine="V"):
-            t = wgrpp.tile([P, 2048], BF16, name="wgrp", tag="wgrp", align_bytes=64)
+        def raw_weights(w, c, g):
+            return wide[c, g][:] if w == "s" else w_raw[w, c, g]
+
+        def interleave(w, c, g, engine):
+            t = grpp.tile([P, 2048], BF16, name="grp", tag="grp", align_bytes=64)
             w_grp[w, c, g] = t
-            src = wide[c, g] if w == "s" else w_raw[w, c, g]
+            src = raw_weights(w, c, g)
             if w in "rs":
-                dst = t[:].rearrange("p (t m j) -> p t m j", t=4, j=4)
-                view = src[:].rearrange("p j (m t) -> p t m j", t=4)
+                dst = t[:].rearrange("p (t m j) -> p m t j", t=4, j=4)
+                move(engine, dst, src.rearrange("p j (m t) -> p m t j", t=4))
             else:
                 dst = t[:].rearrange("p (c i j) -> p c j i", i=4, j=4)
-                view = src[:].rearrange("p j (c i) -> p c j i", i=4)
-            if engine == "V":
-                nc.vector.tensor_copy(dst, view)
-            else:
-                nc.scalar.copy(dst, view)
+                move(engine, dst, src.rearrange("p j (c i) -> p c j i", i=4))
+
+        def interleave_pe(w, c, g, half):
+            src = raw_weights(w, c, g)
+            view = src.rearrange("p j (m t) -> p t m j", t=4) if w in "rs" else src.rearrange("p j (t m) -> p t m j", t=4)
+            bank = psum.tile([P, 2, P, 4], BF16, name="bank", tag="bank")
+            banks["i", w, c, g, half] = bank
+            for q in range(2):
+                nc.tensor.matmul(bank[:, q], lhsT=ident_bf[:], rhs=view[:, 2 * half + q], start=True, stop=True)
+
+        def empty_interleaved(w, c, g, half, engine):
+            if (w, c, g) not in w_grp:
+                w_grp[w, c, g] = grpp.tile([P, 2048], BF16, name="grp", tag="grp", align_bytes=64)
+            bank = banks["i", w, c, g, half][:].rearrange("p q m j -> p (q m j)")
+            move(engine, w_grp[w, c, g][:, half * 1024 : (half + 1) * 1024], bank)
 
         def quant_w(w, c, g):
             quantize(("w", w, c, g), w_grp[w, c, g])
@@ -149,7 +176,7 @@ def tile_cachetocachegatedkeyfuser_kernel(
                     )
 
         def act_silu(g, h, b):
-            if b == 0:
+            if (g, h) not in silu:
                 silu[g, h] = hidp.tile([P, 512, 4], F32, name="silu", tag="silu")
             nc.scalar.activation(
                 out=silu[g, h][:, b * P : (b + 1) * P, :],
@@ -158,7 +185,7 @@ def tile_cachetocachegatedkeyfuser_kernel(
             )
 
         def gain(g, h):
-            t = hidp.tile([P, 2048], BF16, name="hgrp", tag="hgrp", align_bytes=64)
+            t = grpp.tile([P, 2048], BF16, name="grp", tag="grp", align_bytes=64)
             h_grp[g, h] = t
             nc.vector.tensor_tensor(
                 out=t[:].rearrange("p (n t) -> p n t", t=4),
@@ -170,23 +197,20 @@ def tile_cachetocachegatedkeyfuser_kernel(
         def quant_h(g, h):
             quantize(("h", g, h), h_grp[g, h])
 
-        def mm2(h, d, b):
+        def mm2(w, h, d, b):
             cols = slice(b * P, (b + 1) * P)
-            for w in "gd":
-                bank = psum.tile([P, 512], F32, name="bank", tag="bank")
-                banks[w, h, d, b] = bank
-                for c in range(2):
-                    nc.tensor.matmul_mx(
-                        out=bank[:],
-                        lhsT=codes["h", c, h][:, cols].bitcast(FP8X4),
-                        lhsT_scale=scales["h", c, h][:, cols],
-                        rhs=codes["w", w, c, d][:].bitcast(FP8X4),
-                        rhs_scale=scales["w", w, c, d][:],
-                        start=(c == 0),
-                        stop=(c == 1),
-                    )
-
-        gates, prods = {}, {}
+            bank = psum.tile([P, 512], F32, name="bank", tag="bank")
+            banks[w, h, d, b] = bank
+            for c in range(2):
+                nc.tensor.matmul_mx(
+                    out=bank[:],
+                    lhsT=codes["h", c, h][:, cols].bitcast(FP8X4),
+                    lhsT_scale=scales["h", c, h][:, cols],
+                    rhs=codes["w", w, c, d][:].bitcast(FP8X4),
+                    rhs_scale=scales["w", w, c, d][:],
+                    start=(c == 0),
+                    stop=(c == 1),
+                )
 
         def act_gate(h, d, b):
             t = outp.tile([P, 512], F32, name="gate", tag="gate")
@@ -200,135 +224,46 @@ def tile_cachetocachegatedkeyfuser_kernel(
                 out=t[:], in0=gates[h, d, b][:], scalar=1.0, in1=banks["d", h, d, b][:], op0=ALU.add, op1=ALU.mult
             )
 
-        def residual(h, d, b):
-            t = outp.tile([P, 512], F32, name="res", tag="res")
+        def residual(h, d, b, engine):
+            t = resp.tile([P, 512], F32, name="res", tag="res")
             nc.vector.scalar_tensor_tensor(
-                out=t[:], in0=prods[h, d, b][:], scalar=0.5, in1=k_raw["r", d, h][:, b, :], op0=ALU.mult, op1=ALU.add
+                out=t[:],
+                in0=prods[h, d, b][:],
+                scalar=0.5,
+                in1=k_raw["r", h, b // 2][:, b % 2, d * 512 : (d + 1) * 512],
+                op0=ALU.mult,
+                op1=ALU.add,
             )
             r0 = h * 512 + b * P
             nc.sync.dma_start(out=out[r0 : r0 + P, d * 512 : (d + 1) * 512], in_=t[:])
 
         PASSES = (("r", 0), ("s", 0), ("r", 1), ("s", 1))
-
-        def unit(g, h):
-            for b in range(4):
-                mm(g, h, b)
-                act_silu(g, h, b)
-
-        load_b(0, 0)
-        load_w("r", 0, 0)
-        load_k("r", 0, 0)
-        load_b(1, 0)
-        load_w("r", 1, 0)
-        load_k("s", 0, 0)
-        load_k("r", 1, 0)
-        load_k("s", 1, 0)
-        load_b(0, 1)
-        load_b(1, 1)
-        load_w("r", 0, 1)
-        load_w("r", 1, 1)
-        for x in "rs":
-            for c in range(2):
-                load_k(x, c, 1)
-        load_w("d", 0, 0)
-        load_w("g", 0, 0)
-        load_w("d", 1, 0)
-
-        widen(0, 0)
-        interleave("r", 0, 0)
-        transposes("r", 0, 0)
-        empty_transposed("r", 0, 0, "SS")
-        interleave("s", 0, 0)
-        quant_w("r", 0, 0)
-        quant_w("s", 0, 0)
-        widen(1, 0)
-        interleave("r", 1, 0)
-        quant_k("r", 0, 0)
-        transposes("s", 0, 0)
-        empty_transposed("s", 0, 0, "SS")
-        interleave("s", 1, 0)
-        quant_w("r", 1, 0)
-        quant_k("s", 0, 0)
-        transposes("r", 1, 0)
-        empty_transposed("r", 1, 0, "SS")
-        quant_w("s", 1, 0)
-        transposes("s", 1, 0)
-        quant_k("r", 1, 0)
-        empty_transposed("s", 1, 0, "SS")
-        interleave("r", 0, 1)
-        quant_k("s", 1, 0)
-        unit(0, 0)
-        widen(0, 1)
-        interleave("r", 1, 1)
-        quant_w("r", 0, 1)
-        load_w("g", 1, 0)
-        for w, c in (("d", 0), ("g", 0), ("d", 1), ("g", 1)):
-            load_w(w, c, 1)
-        transposes("r", 0, 1)
-        transposes("r", 1, 1)
-        widen(1, 1)
-        quant_w("r", 1, 1)
-        interleave("s", 0, 1)
-        interleave("s", 1, 1)
-        quant_w("s", 0, 1)
-        quant_w("s", 1, 1)
-        unit(1, 0)
-        empty_transposed("r", 0, 1, "SS")
-        gain(0, 0)
-        quant_h(0, 0)
-        empty_transposed("r", 1, 1, "SS")
-        transposes("s", 0, 1)
-        transposes("s", 1, 1)
-        quant_k("r", 0, 1)
-        quant_k("r", 1, 1)
-        interleave("g", 0, 0, "V")
-        empty_transposed("s", 0, 1, "SS")
-        empty_transposed("s", 1, 1, "SS")
-        gain(1, 0)
-        interleave("d", 0, 0, "S")
-        quant_w("g", 0, 0)
-        quant_k("s", 0, 1)
-        quant_k("s", 1, 1)
-        unit(0, 1)
-        quant_h(1, 0)
-        interleave("d", 1, 0, "S")
-        interleave("g", 1, 0, "S")
-        quant_w("d", 0, 0)
-        quant_w("g", 1, 0)
-        quant_w("d", 1, 0)
-        tail = []
-
-        def stage2(h, d, b):
-            mm2(h, d, b)
-            act_gate(h, d, b)
-            tail.append((h, d, b))
-
-        def finish(n):
-            while len(tail) > n:
-                product(*tail[0])
-                residual(*tail[0])
-                tail.remove(tail[0])
-
-        for b in range(4):
-            stage2(0, 0, b)
-            finish(1)
-            if b == 0:
-                gain(0, 1)
-                interleave("d", 0, 1, "S")
-            if b == 1:
-                quant_h(0, 1)
-                quant_w("d", 0, 1)
-        unit(1, 1)
-        interleave("g", 0, 1, "S")
-        interleave("d", 1, 1, "S")
-        quant_w("g", 0, 1)
-        interleave("g", 1, 1, "V")
-        quant_w("d", 1, 1)
-        quant_w("g", 1, 1)
-        gain(1, 1)
-        quant_h(1, 1)
-        for h, d in ((0, 1), (1, 0), (1, 1)):
-            for b in range(4):
-                stage2(h, d, b)
-                finish(1)
-        finish(0)
+        CALLS = {
+            "T": transposes, "E": empty_transposed, "QK": quant_k, "W": widen, "I": interleave, "P": interleave_pe,
+            "C": empty_interleaved, "QW": quant_w, "M": mm, "SI": act_silu, "GM": gain, "QH": quant_h, "X": mm2,
+            "SG": act_gate, "PR": product, "AD": residual,
+        }
+        for n in "Rr00 B0 Kr00 Rr10 Ks00 Kr01 Ks01 B1 Rr01 Rr11 Kr10 Kr11 Ks10 Ks11 Rd0 Rg0 Rd1 Rg1".split():
+            load(n)
+        ORDER = """
+    Pr001 Pr000 Cr001.S W000 Cr000.V QWr00 W001 Tr100 Tr000 W011 Is00.V W010 Ts000 QWs00 Ts100
+    Es000.S Is01.V Tr001 Er100.S Tr101 Er001.S Ts001 Es100.V Er000.S Ts101 Er101.V Es001.S QWs01
+    W110 QKr10 QKr00 W111 QKs00 W100 Es101.V Pr111 Is11.V W101 Pr110 QKs10 Tr010 Ir10.S Cr110.V
+    Tr011 Is10.V Tr110 Ts010 Tr111 Er011.S Cr111.V Ts110 Er110.S QWs10 Ts011 Er010.S QWr10 Ts111
+    Er111.S QKr01 Ir01.S M001 QWr11 QWs11 M002 QKr11 Id00.V Es010.S M000 Es110.S QWr01 Es011.S
+    M003 QWd00 SI001 QKs01 Es111.S M101 Ig01.V SI000 SI002 M103 SI003 QKs11 Ig00.S GM00 M113
+    M111 Id11.V SI101 M110 Id01.S Id10.V M112 QWg01 M010 SI103 QWd01 SI111 QWd11 SI112 M011
+    QWd10 SI113 QWg00 SI110 M100 QH00 Ig10.S GM11 M102 M012 SI100 QWg10 SI102 QH11 M013 SI010
+    GM10 SI011 SI012 SI013 Ig11.S QH10 GM01 Xg000 Xd000 Xg001 SG000 Xd001 SG001 QWg11 Xg002
+    PR000 Xd002 SG002 PR001 Xg003 QH01 Xd003 SG003 AD000.V Xg100 PR002 Xd100 SG100 AD001.V Xg101
+    AD002.V Xd101 SG101 PR003 Xg102 Xd102 PR100 SG102 Xg103 PR101 Xd103 AD003.V SG103 Xg010
+    AD100.V Xd010 PR102 SG010 Xg011 AD101.V Xd011 SG011 PR103 Xg012 AD102.V Xd012 SG012 PR010
+    Xg013 AD103.V Xd013 SG013 PR011 Xg110 PR012 Xd110 SG110 AD010.V Xg111 PR013 Xd111 SG111
+    AD011.V Xg112 AD012.V Xd112 SG112 PR110 Xg113 AD013.V Xd113 SG113 AD110.V PR111 PR112
+    AD111.V PR113 AD112.V AD113.V
+        """
+        for word in ORDER.split():
+            name, engine = (word.split(".") + [""])[:2]
+            key = name[:2] if name[:2] in CALLS else name[:1]
+            args = [int(v) if v in "0123" else v for v in name[len(key) :]]
+            CALLS[key](*args, *([engine] if engine else []))

@@ -4,9 +4,13 @@ import concourse.mybir as mybir
 from concourse.masks import make_identity
 
 T, D, DS, F = 1024, 1024, 1024, 1024
-FLOPS = 2 * T * F * (D + DS) + 2 * 2 * T * F * D
+FLOPS = 2 * T * F * (D + DS) + 2 * T * D * (F + F)
 
 P = 128
+PACK = 4
+HALF = 512
+BLOCKS = HALF // P
+
 F32 = mybir.dt.float32
 BF16 = mybir.dt.bfloat16
 U32 = mybir.dt.uint32
@@ -23,247 +27,343 @@ def tile_cachetocachegatedkeyfuser_kernel(
     nc = tc.nc
     with ExitStack() as ctx:
         keep = ctx.enter_context(tc.tile_pool(name="keep", bufs=1))
-        rawp = ctx.enter_context(tc.tile_pool(name="rawp", bufs=8))
-        grpp = ctx.enter_context(tc.tile_pool(name="grpp", bufs=9))
-        hidp = ctx.enter_context(tc.tile_pool(name="hidp", bufs=2))
-        outp = ctx.enter_context(tc.tile_pool(name="outp", bufs=3))
-        resp = ctx.enter_context(tc.tile_pool(name="resp", bufs=5))
+        raw_pool = ctx.enter_context(tc.tile_pool(name="raw_pool", bufs=5))
+        wide_pool = ctx.enter_context(tc.tile_pool(name="wide_pool", bufs=3))
+        grouped_pool = ctx.enter_context(tc.tile_pool(name="grouped_pool", bufs=9))
+        silu_pool = ctx.enter_context(tc.tile_pool(name="silu_pool", bufs=2))
+        gate_pool = ctx.enter_context(tc.tile_pool(name="gate_pool", bufs=3))
+        out_pool = ctx.enter_context(tc.tile_pool(name="out_pool", bufs=5))
         psum = ctx.enter_context(tc.psum_pool(name="psum", bufs=8))
-
         ctx.enter_context(tc.manual_schedule())
-        k_view = {
-            "r": k_recv.rearrange("(h i b r) k -> h i r b k", h=2, i=2, r=P),
-            "s": k_share.rearrange("(h i b r) k -> h i r b k", h=2, i=2, r=P),
+
+
+        scale_sb = keep.tile([P, 2, PACK], F32, name="scale_sb")
+        nc.scalar.dma_start(out=scale_sb[:], in_=w_share_scale.rearrange("(c p j) o -> p c (j o)", p=P, j=PACK))
+        gain_sb = keep.tile([P, 2, PACK], BF16, name="gain_sb")
+        nc.scalar.dma_start(out=gain_sb[:], in_=g_hid.rearrange("(g p t) -> p g t", p=P, t=PACK))
+        zero = keep.tile([P, 1], F32, name="zero")
+        nc.gpsimd.memset(zero[:], 0.0)
+        unread = keep.tile([P, 1], F32, name="unread")
+        nc.scalar.activation(out=unread[:], in_=zero[:], func=ACT.Silu)
+        identity = keep.tile([P, P], F32, name="identity")
+        make_identity(nc, identity[:])
+        identity_bf16 = keep.tile([P, P], BF16, name="identity_bf16")
+        nc.gpsimd.tensor_copy(out=identity_bf16[:], in_=identity[:])
+
+
+        keys_hbm = {
+            "recv": k_recv.rearrange("(h i b r) k -> h i r b k", h=2, i=2, r=P),
+            "share": k_share.rearrange("(h i b r) k -> h i r b k", h=2, i=2, r=P),
         }
-        w_view = {
-            "r": w_recv.rearrange("(c p j) (g n) -> c g p j n", p=P, j=4, g=2),
-            "d": w_delta.rearrange("(c p j) n -> c p j n", p=P, j=4),
-            "g": w_gate.rearrange("(c p j) n -> c p j n", p=P, j=4),
+        recv_hbm = w_recv.rearrange("(c p j) (g n) -> c g p j n", p=P, j=PACK, g=2)
+        bytes_hbm = w_share_bytes.rearrange("(c p j) n -> c p j n", p=P, j=PACK)
+        stage2_hbm = {
+            "delta": w_delta.rearrange("(c p j) n -> c p j n", p=P, j=PACK),
+            "gate": w_gate.rearrange("(c p j) n -> c p j n", p=P, j=PACK),
         }
-        b_view = w_share_bytes.rearrange("(c p j) n -> c p j n", p=P, j=4)
+        keys, weights, share_bytes = {}, {}, {}
 
-        k_raw, w_raw, b_raw = {}, {}, {}
-        wide, w_grp, k_grp = {}, {}, {}
-        codes, scales = {}, {}
-        banks, silu, h_grp = {}, {}, {}
-        gates, prods = {}, {}
-
-        def load(n):
-            if n[0] == "K":
-                x, h, i = n[1], int(n[2]), int(n[3])
-                if x == "r":
-                    t = keep.tile([P, 2, 1024], BF16, name="k_" + n)
-                else:
-                    t = rawp.tile([P, 4, 512], BF16, name="raw", tag="raw")
-                    t = t[:].rearrange("p a b -> p (a b)").rearrange("p (b k) -> p b k", b=2)
-                k_raw[x, h, i] = t
-                nc.sync.dma_start(out=t[:], in_=k_view[x][h, i])
-            elif n[0] == "B":
-                t = keep.tile([P, 4, 1024], U8, name="bytes" + n[1])
-                b_raw[int(n[1])] = t
-                nc.sync.dma_start(out=t[:], in_=b_view[int(n[1])])
-            elif n[1] == "r":
-                c, g = int(n[2]), int(n[3])
-                t = rawp.tile([P, 4, 512], BF16, name="raw", tag="raw")
-                w_raw["r", c, g] = t[:]
-                nc.sync.dma_start(out=t[:], in_=w_view["r"][c, g])
+        def load_keys(name, h, i):
+            if name == "recv":
+                tile = keep.tile([P, 2, D], BF16, name=f"recv_keys_{h}{i}")
             else:
-                c = int(n[2])
-                t = keep.tile([P, 4, 1024], BF16, name="w_" + n)
-                for g in range(2):
-                    w_raw[n[1], c, g] = t[:, :, g * 512 : (g + 1) * 512]
-                nc.sync.dma_start(out=t[:], in_=w_view[n[1]][c])
+                tile = raw_pool.tile([P, 2, DS], BF16, name="raw", tag="raw")
+            keys[name, h, i] = tile
+            nc.sync.dma_start(out=tile[:], in_=keys_hbm[name][h, i])
 
-        scale_sb = keep.tile([P, 2, 4], F32, name="scale_sb")
-        nc.scalar.dma_start(out=scale_sb[:], in_=w_share_scale.rearrange("(c p j) o -> p c (j o)", p=P, j=4))
-        gain_sb = keep.tile([P, 2, 4], BF16, name="gain_sb")
-        nc.scalar.dma_start(out=gain_sb[:], in_=g_hid.rearrange("(g p t) -> p g t", p=P, t=4))
-        warm = keep.tile([P, 1], F32, name="warm")
-        nc.gpsimd.memset(warm[:], 0.0)
-        warm2 = keep.tile([P, 1], F32, name="warm2")
-        nc.scalar.activation(out=warm2[:], in_=warm[:], func=ACT.Silu)
-        ident = keep.tile([P, P], F32, name="ident")
-        make_identity(nc, ident[:])
-        ident_bf = keep.tile([P, P], BF16, name="ident_bf")
-        nc.gpsimd.tensor_copy(out=ident_bf[:], in_=ident[:])
+        def load_recv_weights(c, g, columns):
+            if ("recv", c, g) not in weights:
+                tile = raw_pool.tile([P, PACK, HALF], BF16, name="raw", tag="raw")
+                weights["recv", c, g] = tile[:]
+            nc.sync.dma_start(out=weights["recv", c, g][:, :, columns], in_=recv_hbm[c, g][:, :, columns])
 
-        def move(engine, dst, src):
-            if engine == "S":
-                nc.scalar.copy(dst, src)
+        def load_share_bytes(c, rows):
+            if c not in share_bytes:
+                share_bytes[c] = keep.tile([P, PACK, F], U8, name=f"share_bytes_{c}")
+            nc.sync.dma_start(out=share_bytes[c][:, rows, :], in_=bytes_hbm[c][:, rows, :])
+
+        def load_stage2_weights(name, c):
+            tile = keep.tile([P, PACK, D], BF16, name=f"{name}_weights_{c}")
+            for d in range(2):
+                weights[name, c, d] = tile[:, :, d * HALF : (d + 1) * HALF]
+            nc.sync.dma_start(out=tile[:], in_=stage2_hbm[name][c])
+
+
+        grouped, codes, scales = {}, {}, {}
+
+        def new_grouped(key):
+            grouped[key] = grouped_pool.tile([P, PACK * HALF], BF16, name="grouped", tag="grouped", align_bytes=64)
+            return grouped[key]
+
+        def quantize(*key):
+            label = "_".join(str(part) for part in key)
+            codes[key] = keep.tile([P, HALF], U32, name="codes_" + label, align_bytes=64)
+            scales[key] = keep.tile([P, HALF], U8, name="scales_" + label, align_bytes=64)
+            nc.vector.quantize_mx(out=codes[key][:].bitcast(FP8X4), scales=scales[key][:], in_=grouped[key][:])
+
+        def copy(engine, out_view, in_view):
+            if engine is nc.scalar:
+                nc.scalar.copy(out_view, in_view)
             else:
-                nc.vector.tensor_copy(dst, src)
+                nc.vector.tensor_copy(out_view, in_view)
 
-        def transposes(x, c, h, i):
-            words = k_raw[x, h, i][:].bitcast(F32)
-            bank = psum.tile([P, 2, 2, P], F32, name="bank", tag="bank")
-            banks["t", x, c, h, i] = bank
-            for b in range(2):
-                for u in range(2):
-                    nc.tensor.transpose(bank[:, b, u, :], words[:, b, c * 256 + u : (c + 1) * 256 : 2], ident[:])
 
-        def empty_transposed(x, c, h, i, engine):
-            if (x, c, h) not in k_grp:
-                k_grp[x, c, h] = grpp.tile([P, 2048], BF16, name="grp", tag="grp", align_bytes=64)
-            dst = k_grp[x, c, h][:].bitcast(F32).rearrange("p (i b r u) -> p i b r u", i=2, b=2, u=2)
-            move(engine, dst[:, i], banks["t", x, c, h, i][:].rearrange("p b u r -> p b r u"))
+        turned = {}
 
-        def quantize(key, src):
-            cd = keep.tile([P, 512], U32, name="cd_" + "_".join(str(v) for v in key), align_bytes=64)
-            sc = keep.tile([P, 512], U8, name="sc_" + "_".join(str(v) for v in key), align_bytes=64)
-            codes[key], scales[key] = cd, sc
-            nc.vector.quantize_mx(out=cd[:].bitcast(FP8X4), scales=sc[:], in_=src[:])
+        def transpose_keys(name, h, i):
+            words = keys[name, h, i][:].bitcast(F32)
+            for c in range(2):
+                bank = psum.tile([P, 2, 2, P], F32, name="bank", tag="bank")
+                turned[name, c, h, i] = bank
+                for b in range(2):
+                    for u in range(2):
+                        pair = words[:, b, c * 256 + u : (c + 1) * 256 : 2]
+                        nc.tensor.transpose(bank[:, b, u, :], pair, identity[:])
 
-        def quant_k(x, c, h):
-            quantize(("k", x, c, h), k_grp[x, c, h])
+        def group_keys(engine, name, c, h, i):
+            key = ("keys", name, c, h)
+            if key not in grouped:
+                new_grouped(key)
+            out_words = grouped[key][:].bitcast(F32).rearrange("p (i b r u) -> p i b r u", i=2, b=2, u=2)
+            copy(engine, out_words[:, i], turned[name, c, h, i][:].rearrange("p b u r -> p b r u"))
 
-        def widen(c, g, half):
-            if (c, g) not in wide:
-                wide[c, g] = rawp.tile([P, 4, 512], BF16, name="raw", tag="raw")
-            for j in (2 * half, 2 * half + 1):
+
+        def widen(c, g):
+            tile = wide_pool.tile([P, PACK, HALF], BF16, name="wide", tag="wide")
+            weights["share", c, g] = tile[:]
+            for j in range(PACK):
                 nc.scalar.activation(
-                    out=wide[c, g][:, j, :],
-                    in_=b_raw[c][:, j, g * 512 : (g + 1) * 512].bitcast(FP8),
+                    out=tile[:, j, :],
+                    in_=share_bytes[c][:, j, g * HALF : (g + 1) * HALF].bitcast(FP8),
                     func=ACT.Copy,
                     scale=scale_sb[:, c, j : j + 1],
                 )
 
-        def raw_weights(w, c, g):
-            return wide[c, g][:] if w == "s" else w_raw[w, c, g]
+        def group_permuted(engine, name, c, g, columns=slice(0, P)):
+            key = ("weights", name, c, g)
+            if key not in grouped:
+                new_grouped(key)
+            out_view = grouped[key][:].rearrange("p (t m j) -> p m t j", t=BLOCKS, j=PACK)
+            in_view = weights[name, c, g].rearrange("p j (m t) -> p m t j", t=BLOCKS)
+            copy(engine, out_view[:, columns], in_view[:, columns])
 
-        def interleave(w, c, g, engine):
-            t = grpp.tile([P, 2048], BF16, name="grp", tag="grp", align_bytes=64)
-            w_grp[w, c, g] = t
-            src = raw_weights(w, c, g)
-            if w in "rs":
-                dst = t[:].rearrange("p (t m j) -> p m t j", t=4, j=4)
-                move(engine, dst, src.rearrange("p j (m t) -> p m t j", t=4))
-            else:
-                dst = t[:].rearrange("p (c i j) -> p c j i", i=4, j=4)
-                move(engine, dst, src.rearrange("p j (c i) -> p c j i", i=4))
+        def group_plain(engine, name, c, d):
+            out_view = new_grouped(("weights", name, c, d))[:].rearrange("p (q i j) -> p q j i", i=4, j=PACK)
+            copy(engine, out_view, weights[name, c, d].rearrange("p j (q i) -> p q j i", i=4))
 
-        def interleave_pe(w, c, g, half):
-            src = raw_weights(w, c, g)
-            view = src.rearrange("p j (m t) -> p t m j", t=4) if w in "rs" else src.rearrange("p j (t m) -> p t m j", t=4)
-            bank = psum.tile([P, 2, P, 4], BF16, name="bank", tag="bank")
-            banks["i", w, c, g, half] = bank
-            for q in range(2):
-                nc.tensor.matmul(bank[:, q], lhsT=ident_bf[:], rhs=view[:, 2 * half + q], start=True, stop=True)
+        permuted_banks = {}
 
-        def empty_interleaved(w, c, g, half, engine):
-            if (w, c, g) not in w_grp:
-                w_grp[w, c, g] = grpp.tile([P, 2048], BF16, name="grp", tag="grp", align_bytes=64)
-            bank = banks["i", w, c, g, half][:].rearrange("p q m j -> p (q m j)")
-            move(engine, w_grp[w, c, g][:, half * 1024 : (half + 1) * 1024], bank)
-
-        def quant_w(w, c, g):
-            quantize(("w", w, c, g), w_grp[w, c, g])
-
-        def mm(g, h, b):
-            bank = psum.tile([P, 4, P], F32, name="bank", tag="bank")
-            banks["u", g, h, b] = bank
-            tokens = slice(b * P, (b + 1) * P)
-            for t in range(4):
-                cols = slice(t * P, (t + 1) * P)
-                for x, c in PASSES:
-                    nc.tensor.matmul_mx(
-                        out=bank[:, t],
-                        lhsT=codes["w", x, c, g][:, cols].bitcast(FP8X4),
-                        lhsT_scale=scales["w", x, c, g][:, cols],
-                        rhs=codes["k", x, c, h][:, tokens].bitcast(FP8X4),
-                        rhs_scale=scales["k", x, c, h][:, tokens],
-                        start=(x, c) == PASSES[0],
-                        stop=(x, c) == PASSES[-1],
+        def permute_on_tensor(name, c, g):
+            in_view = weights[name, c, g].rearrange("p j (m t) -> p t m j", t=BLOCKS)
+            for half in range(2):
+                bank = psum.tile([P, 2, P, PACK], BF16, name="bank", tag="bank")
+                permuted_banks[name, c, g, half] = bank
+                for q in range(2):
+                    nc.tensor.matmul(
+                        bank[:, q], lhsT=identity_bf16[:], rhs=in_view[:, 2 * half + q], start=True, stop=True
                     )
 
-        def act_silu(g, h, b):
-            if (g, h) not in silu:
-                silu[g, h] = hidp.tile([P, 512, 4], F32, name="silu", tag="silu")
-            nc.scalar.activation(
-                out=silu[g, h][:, b * P : (b + 1) * P, :],
-                in_=banks["u", g, h, b][:].rearrange("p t n -> p n t"),
-                func=ACT.Silu,
-            )
+        def empty_permuted(engine, name, c, g):
+            tile = new_grouped(("weights", name, c, g))
+            width = PACK * HALF // 2
+            for half in range(2):
+                bank = permuted_banks[name, c, g, half][:].rearrange("p q m j -> p (q m j)")
+                copy(engine, tile[:, half * width : (half + 1) * width], bank)
+
+
+        silu = {}
+        PASSES = (("recv", 0), ("share", 0), ("recv", 1), ("share", 1))
+
+        def hidden(g, h):
+            silu[g, h] = silu_pool.tile([P, HALF, PACK], F32, name="silu", tag="silu")
+            for b in range(BLOCKS):
+                tokens = slice(b * P, (b + 1) * P)
+                bank = psum.tile([P, BLOCKS, P], F32, name="bank", tag="bank")
+                for t in range(BLOCKS):
+                    channels = slice(t * P, (t + 1) * P)
+                    for name, c in PASSES:
+                        weight_key, key_key = ("weights", name, c, g), ("keys", name, c, h)
+                        nc.tensor.matmul_mx(
+                            out=bank[:, t],
+                            lhsT=codes[weight_key][:, channels].bitcast(FP8X4),
+                            lhsT_scale=scales[weight_key][:, channels],
+                            rhs=codes[key_key][:, tokens].bitcast(FP8X4),
+                            rhs_scale=scales[key_key][:, tokens],
+                            start=(name, c) == PASSES[0],
+                            stop=(name, c) == PASSES[-1],
+                        )
+                nc.scalar.activation(
+                    out=silu[g, h][:, tokens, :], in_=bank[:].rearrange("p t n -> p n t"), func=ACT.Silu
+                )
 
         def gain(g, h):
-            t = grpp.tile([P, 2048], BF16, name="grp", tag="grp", align_bytes=64)
-            h_grp[g, h] = t
             nc.vector.tensor_tensor(
-                out=t[:].rearrange("p (n t) -> p n t", t=4),
+                out=new_grouped(("hidden", g, h))[:].rearrange("p (n t) -> p n t", t=PACK),
                 in0=silu[g, h][:],
-                in1=gain_sb[:, g : g + 1, :].to_broadcast([P, 512, 4]),
+                in1=gain_sb[:, g : g + 1, :].to_broadcast([P, HALF, PACK]),
                 op=ALU.mult,
             )
 
-        def quant_h(g, h):
-            quantize(("h", g, h), h_grp[g, h])
 
-        def mm2(w, h, d, b):
-            cols = slice(b * P, (b + 1) * P)
-            bank = psum.tile([P, 512], F32, name="bank", tag="bank")
-            banks[w, h, d, b] = bank
+        sums, tanh, gates, products = {}, {}, {}, {}
+
+        def contract_hidden(name, h, d, b):
+            tokens = slice(b * P, (b + 1) * P)
+            sums[name, h, d, b] = psum.tile([P, HALF], F32, name="bank", tag="bank")
             for c in range(2):
                 nc.tensor.matmul_mx(
-                    out=bank[:],
-                    lhsT=codes["h", c, h][:, cols].bitcast(FP8X4),
-                    lhsT_scale=scales["h", c, h][:, cols],
-                    rhs=codes["w", w, c, d][:].bitcast(FP8X4),
-                    rhs_scale=scales["w", w, c, d][:],
+                    out=sums[name, h, d, b][:],
+                    lhsT=codes["hidden", c, h][:, tokens].bitcast(FP8X4),
+                    lhsT_scale=scales["hidden", c, h][:, tokens],
+                    rhs=codes["weights", name, c, d][:].bitcast(FP8X4),
+                    rhs_scale=scales["weights", name, c, d][:],
                     start=(c == 0),
                     stop=(c == 1),
                 )
 
-        def act_gate(h, d, b):
-            t = outp.tile([P, 512], F32, name="gate", tag="gate")
-            gates[h, d, b] = t
-            nc.scalar.activation(out=t[:], in_=banks["g", h, d, b][:], func=ACT.Tanh, scale=0.5)
+        def on_gpsimd(h, d, b):
+            return b == 1 and (h, d) != (0, 0)
+
+        def gate(h, d, b):
+            tanh[h, d, b] = gate_pool.tile([P, HALF], F32, name="gate", tag="gate")
+            nc.scalar.activation(out=tanh[h, d, b][:], in_=sums["gate", h, d, b][:], func=ACT.Tanh, scale=0.5)
+            if on_gpsimd(h, d, b):
+                gates[h, d, b] = gate_pool.tile([P, HALF], F32, name="gate", tag="gate")
+                nc.scalar.activation(
+                    out=gates[h, d, b][:], in_=tanh[h, d, b][:], func=ACT.Identity, scale=0.5, bias=0.5
+                )
 
         def product(h, d, b):
-            t = outp.tile([P, 512], F32, name="prod", tag="prod")
-            prods[h, d, b] = t
-            nc.vector.scalar_tensor_tensor(
-                out=t[:], in0=gates[h, d, b][:], scalar=1.0, in1=banks["d", h, d, b][:], op0=ALU.add, op1=ALU.mult
-            )
+            products[h, d, b] = gate_pool.tile([P, HALF], F32, name="product", tag="product")
+            delta = sums["delta", h, d, b][:]
+            if on_gpsimd(h, d, b):
+                nc.vector.tensor_tensor(out=products[h, d, b][:], in0=delta, in1=gates[h, d, b][:], op=ALU.mult)
+            else:
+                nc.vector.scalar_tensor_tensor(
+                    out=products[h, d, b][:], in0=tanh[h, d, b][:], scalar=1.0, in1=delta, op0=ALU.add, op1=ALU.mult
+                )
 
-        def residual(h, d, b, engine):
-            t = resp.tile([P, 512], F32, name="res", tag="res")
-            nc.vector.scalar_tensor_tensor(
-                out=t[:],
-                in0=prods[h, d, b][:],
-                scalar=0.5,
-                in1=k_raw["r", h, b // 2][:, b % 2, d * 512 : (d + 1) * 512],
-                op0=ALU.mult,
-                op1=ALU.add,
-            )
-            r0 = h * 512 + b * P
-            nc.sync.dma_start(out=out[r0 : r0 + P, d * 512 : (d + 1) * 512], in_=t[:])
+        def residual(h, d, b):
+            result = out_pool.tile([P, HALF], F32, name="result", tag="result")
+            columns = slice(d * HALF, (d + 1) * HALF)
+            recv = keys["recv", h, b // 2][:, b % 2, columns]
+            if on_gpsimd(h, d, b):
+                nc.gpsimd.tensor_tensor(out=result[:], in0=products[h, d, b][:], in1=recv, op=ALU.add)
+            else:
+                nc.vector.scalar_tensor_tensor(
+                    out=result[:], in0=products[h, d, b][:], scalar=0.5, in1=recv, op0=ALU.mult, op1=ALU.add
+                )
+            first = h * HALF + b * P
+            nc.sync.dma_start(out=out[first : first + P, columns], in_=result[:])
 
-        PASSES = (("r", 0), ("s", 0), ("r", 1), ("s", 1))
-        CALLS = {
-            "T": transposes, "E": empty_transposed, "QK": quant_k, "W": widen, "I": interleave, "P": interleave_pe,
-            "C": empty_interleaved, "QW": quant_w, "M": mm, "SI": act_silu, "GM": gain, "QH": quant_h, "X": mm2,
-            "SG": act_gate, "PR": product, "AD": residual,
-        }
-        for n in "Rr00 B0 Kr00 Rr10 Ks00 Kr01 Ks01 B1 Rr01 Rr11 Kr10 Kr11 Ks10 Ks11 Rd0 Rg0 Rd1 Rg1".split():
-            load(n)
-        ORDER = """
-    Pr001 Pr000 Cr001.S W000 Cr000.V QWr00 W001 Tr100 Tr000 W011 Is00.V W010 Ts000 QWs00 Ts100
-    Es000.S Is01.V Tr001 Er100.S Tr101 Er001.S Ts001 Es100.V Er000.S Ts101 Er101.V Es001.S QWs01
-    W110 QKr10 QKr00 W111 QKs00 W100 Es101.V Pr111 Is11.V W101 Pr110 QKs10 Tr010 Ir10.S Cr110.V
-    Tr011 Is10.V Tr110 Ts010 Tr111 Er011.S Cr111.V Ts110 Er110.S QWs10 Ts011 Er010.S QWr10 Ts111
-    Er111.S QKr01 Ir01.S M001 QWr11 QWs11 M002 QKr11 Id00.V Es010.S M000 Es110.S QWr01 Es011.S
-    M003 QWd00 SI001 QKs01 Es111.S M101 Ig01.V SI000 SI002 M103 SI003 QKs11 Ig00.S GM00 M113
-    M111 Id11.V SI101 M110 Id01.S Id10.V M112 QWg01 M010 SI103 QWd01 SI111 QWd11 SI112 M011
-    QWd10 SI113 QWg00 SI110 M100 QH00 Ig10.S GM11 M102 M012 SI100 QWg10 SI102 QH11 M013 SI010
-    GM10 SI011 SI012 SI013 Ig11.S QH10 GM01 Xg000 Xd000 Xg001 SG000 Xd001 SG001 QWg11 Xg002
-    PR000 Xd002 SG002 PR001 Xg003 QH01 Xd003 SG003 AD000.V Xg100 PR002 Xd100 SG100 AD001.V Xg101
-    AD002.V Xd101 SG101 PR003 Xg102 Xd102 PR100 SG102 Xg103 PR101 Xd103 AD003.V SG103 Xg010
-    AD100.V Xd010 PR102 SG010 Xg011 AD101.V Xd011 SG011 PR103 Xg012 AD102.V Xd012 SG012 PR010
-    Xg013 AD103.V Xd013 SG013 PR011 Xg110 PR012 Xd110 SG110 AD010.V Xg111 PR013 Xd111 SG111
-    AD011.V Xg112 AD012.V Xd112 SG112 PR110 Xg113 AD013.V Xd113 SG113 AD110.V PR111 PR112
-    AD111.V PR113 AD112.V AD113.V
-        """
-        for word in ORDER.split():
-            name, engine = (word.split(".") + [""])[:2]
-            key = name[:2] if name[:2] in CALLS else name[:1]
-            args = [int(v) if v in "0123" else v for v in name[len(key) :]]
-            CALLS[key](*args, *([engine] if engine else []))
+
+        V, S = nc.vector, nc.scalar
+        everything = slice(0, HALF)
+
+        load_recv_weights(0, 0, slice(0, 256))
+        load_share_bytes(0, slice(0, 2))
+        load_recv_weights(0, 0, slice(256, 512))
+        load_share_bytes(0, slice(2, 4))
+        load_recv_weights(1, 0, everything)
+        for i in range(2):
+            load_keys("recv", 0, i)
+            load_keys("share", 0, i)
+        load_share_bytes(1, slice(0, 4))
+        for c in range(2):
+            load_recv_weights(c, 1, everything)
+        for name in ("recv", "share"):
+            for i in range(2):
+                load_keys(name, 1, i)
+        for c in range(2):
+            for name in ("delta", "gate"):
+                load_stage2_weights(name, c)
+
+        group_permuted(V, "recv", 0, 0, columns=slice(0, 64))
+        group_permuted(V, "recv", 0, 0, columns=slice(64, 128))
+        widen(0, 0)
+        quantize("weights", "recv", 0, 0)
+        group_permuted(S, "share", 0, 0)
+        permute_on_tensor("recv", 1, 0)
+        empty_permuted(V, "recv", 1, 0)
+        widen(0, 1)
+        for i in range(2):
+            transpose_keys("recv", 0, i)
+            transpose_keys("share", 0, i)
+        quantize("weights", "share", 0, 0)
+        quantize("weights", "recv", 1, 0)
+        for c in range(2):
+            group_keys(V, "recv", c, 0, 0)
+            group_keys(S, "share", c, 0, 0)
+        group_keys(V, "recv", 1, 0, 1)
+        group_keys(S, "recv", 0, 0, 1)
+        quantize("keys", "recv", 1, 0)
+        group_keys(V, "share", 1, 0, 1)
+        widen(1, 0)
+        group_keys(S, "share", 0, 0, 1)
+        quantize("keys", "recv", 0, 0)
+        quantize("keys", "share", 1, 0)
+
+        group_permuted(V, "recv", 0, 1)
+        quantize("keys", "share", 0, 0)
+        widen(1, 1)
+        group_permuted(V, "share", 1, 0)
+        permute_on_tensor("recv", 1, 1)
+        empty_permuted(S, "recv", 1, 1)
+        quantize("weights", "recv", 0, 1)
+        group_permuted(V, "share", 1, 1)
+        quantize("weights", "share", 1, 0)
+        quantize("weights", "share", 1, 1)
+        for name in ("recv", "share"):
+            for i in range(2):
+                transpose_keys(name, 1, i)
+                for c in range(2):
+                    group_keys(S, name, c, 1, i)
+        group_permuted(S, "share", 0, 1)
+        quantize("keys", "recv", 0, 1)
+        quantize("keys", "recv", 1, 1)
+        quantize("weights", "recv", 1, 1)
+        group_plain(V, "delta", 0, 1)
+        quantize("keys", "share", 0, 1)
+        quantize("keys", "share", 1, 1)
+        quantize("weights", "delta", 0, 1)
+        quantize("weights", "share", 0, 1)
+        group_plain(V, "gate", 0, 1)
+
+        hidden(0, 0)
+        group_plain(S, "delta", 0, 0)
+        gain(0, 0)
+        group_plain(V, "delta", 1, 0)
+        quantize("hidden", 0, 0)
+        quantize("weights", "delta", 0, 0)
+        quantize("weights", "gate", 0, 1)
+        quantize("weights", "delta", 1, 0)
+        group_plain(V, "gate", 1, 1)
+        hidden(0, 1)
+        group_plain(S, "gate", 1, 0)
+        gain(0, 1)
+        hidden(1, 0)
+        group_plain(S, "gate", 0, 0)
+        gain(1, 0)
+        quantize("weights", "gate", 1, 0)
+        quantize("weights", "gate", 0, 0)
+        quantize("hidden", 1, 0)
+        quantize("hidden", 0, 1)
+        quantize("weights", "gate", 1, 1)
+        hidden(1, 1)
+        gain(1, 1)
+
+        steps = [(h, d, b) for d in range(2) for h in range(2) for b in range(BLOCKS)]
+        for n, step in enumerate(steps):
+            contract_hidden("gate", *step)
+            contract_hidden("delta", *step)
+            gate(*step)
+            product(*step)
+            if n == 0:
+                quantize("hidden", 1, 1)
+            if n == 2:
+                group_plain(S, "delta", 1, 1)
+            if n == 5:
+                quantize("weights", "delta", 1, 1)
+            if n > 0:
+                residual(*steps[n - 1])
+        residual(*steps[-1])

from contextlib import ExitStack

import concourse.mybir as mybir
from concourse.masks import make_identity

T, D, DS, F = 1024, 1024, 1024, 1024
FLOPS = 2 * T * F * (D + DS) + 2 * T * D * (F + F)

P = 128
PACK = 4
HALF = 512
BLOCKS = HALF // P

F32 = mybir.dt.float32
BF16 = mybir.dt.bfloat16
U32 = mybir.dt.uint32
U8 = mybir.dt.uint8
FP8 = mybir.dt.float8_e4m3fn
FP8X4 = mybir.dt.float8_e4m3fn_x4
ACT = mybir.ActivationFunctionType
ALU = mybir.AluOpType


def tile_cachetocachegatedkeyfuser_kernel(
    tc, k_recv, k_share, w_recv, w_share_bytes, w_share_scale, g_hid, w_delta, w_gate, out
):
    nc = tc.nc
    with ExitStack() as ctx:
        keep = ctx.enter_context(tc.tile_pool(name="keep", bufs=1))
        raw_pool = ctx.enter_context(tc.tile_pool(name="raw_pool", bufs=5))
        wide_pool = ctx.enter_context(tc.tile_pool(name="wide_pool", bufs=3))
        grouped_pool = ctx.enter_context(tc.tile_pool(name="grouped_pool", bufs=9))
        silu_pool = ctx.enter_context(tc.tile_pool(name="silu_pool", bufs=2))
        gate_pool = ctx.enter_context(tc.tile_pool(name="gate_pool", bufs=3))
        out_pool = ctx.enter_context(tc.tile_pool(name="out_pool", bufs=5))
        psum = ctx.enter_context(tc.psum_pool(name="psum", bufs=8))
        ctx.enter_context(tc.manual_schedule())


        scale_sb = keep.tile([P, 2, PACK], F32, name="scale_sb")
        nc.scalar.dma_start(out=scale_sb[:], in_=w_share_scale.rearrange("(c p j) o -> p c (j o)", p=P, j=PACK))
        gain_sb = keep.tile([P, 2, PACK], BF16, name="gain_sb")
        nc.scalar.dma_start(out=gain_sb[:], in_=g_hid.rearrange("(g p t) -> p g t", p=P, t=PACK))
        zero = keep.tile([P, 1], F32, name="zero")
        nc.gpsimd.memset(zero[:], 0.0)
        unread = keep.tile([P, 1], F32, name="unread")
        nc.scalar.activation(out=unread[:], in_=zero[:], func=ACT.Silu)
        identity = keep.tile([P, P], F32, name="identity")
        make_identity(nc, identity[:])
        identity_bf16 = keep.tile([P, P], BF16, name="identity_bf16")
        nc.gpsimd.tensor_copy(out=identity_bf16[:], in_=identity[:])


        keys_hbm = {
            "recv": k_recv.rearrange("(h i b r) k -> h i r b k", h=2, i=2, r=P),
            "share": k_share.rearrange("(h i b r) k -> h i r b k", h=2, i=2, r=P),
        }
        recv_hbm = w_recv.rearrange("(c p j) (g n) -> c g p j n", p=P, j=PACK, g=2)
        bytes_hbm = w_share_bytes.rearrange("(c p j) n -> c p j n", p=P, j=PACK)
        stage2_hbm = {
            "delta": w_delta.rearrange("(c p j) n -> c p j n", p=P, j=PACK),
            "gate": w_gate.rearrange("(c p j) n -> c p j n", p=P, j=PACK),
        }
        keys, weights, share_bytes = {}, {}, {}

        def load_keys(name, h, i):
            if name == "recv":
                tile = keep.tile([P, 2, D], BF16, name=f"recv_keys_{h}{i}")
            else:
                tile = raw_pool.tile([P, 2, DS], BF16, name="raw", tag="raw")
            keys[name, h, i] = tile
            nc.sync.dma_start(out=tile[:], in_=keys_hbm[name][h, i])

        def load_recv_weights(c, g, columns):
            if ("recv", c, g) not in weights:
                tile = raw_pool.tile([P, PACK, HALF], BF16, name="raw", tag="raw")
                weights["recv", c, g] = tile[:]
            nc.sync.dma_start(out=weights["recv", c, g][:, :, columns], in_=recv_hbm[c, g][:, :, columns])

        def load_share_bytes(c, rows):
            if c not in share_bytes:
                share_bytes[c] = keep.tile([P, PACK, F], U8, name=f"share_bytes_{c}")
            nc.sync.dma_start(out=share_bytes[c][:, rows, :], in_=bytes_hbm[c][:, rows, :])

        def load_stage2_weights(name, c):
            tile = keep.tile([P, PACK, D], BF16, name=f"{name}_weights_{c}")
            for d in range(2):
                weights[name, c, d] = tile[:, :, d * HALF : (d + 1) * HALF]
            nc.sync.dma_start(out=tile[:], in_=stage2_hbm[name][c])


        grouped, codes, scales = {}, {}, {}

        def new_grouped(key):
            grouped[key] = grouped_pool.tile([P, PACK * HALF], BF16, name="grouped", tag="grouped", align_bytes=64)
            return grouped[key]

        def quantize(*key):
            label = "_".join(str(part) for part in key)
            codes[key] = keep.tile([P, HALF], U32, name="codes_" + label, align_bytes=64)
            scales[key] = keep.tile([P, HALF], U8, name="scales_" + label, align_bytes=64)
            nc.vector.quantize_mx(out=codes[key][:].bitcast(FP8X4), scales=scales[key][:], in_=grouped[key][:])

        def copy(engine, out_view, in_view):
            if engine is nc.scalar:
                nc.scalar.copy(out_view, in_view)
            else:
                nc.vector.tensor_copy(out_view, in_view)


        turned = {}

        def transpose_keys(name, h, i):
            words = keys[name, h, i][:].bitcast(F32)
            for c in range(2):
                bank = psum.tile([P, 2, 2, P], F32, name="bank", tag="bank")
                turned[name, c, h, i] = bank
                for b in range(2):
                    for u in range(2):
                        pair = words[:, b, c * 256 + u : (c + 1) * 256 : 2]
                        nc.tensor.transpose(bank[:, b, u, :], pair, identity[:])

        def group_keys(engine, name, c, h, i):
            key = ("keys", name, c, h)
            if key not in grouped:
                new_grouped(key)
            out_words = grouped[key][:].bitcast(F32).rearrange("p (i b r u) -> p i b r u", i=2, b=2, u=2)
            copy(engine, out_words[:, i], turned[name, c, h, i][:].rearrange("p b u r -> p b r u"))


        def widen(c, g):
            tile = wide_pool.tile([P, PACK, HALF], BF16, name="wide", tag="wide")
            weights["share", c, g] = tile[:]
            for j in range(PACK):
                nc.scalar.activation(
                    out=tile[:, j, :],
                    in_=share_bytes[c][:, j, g * HALF : (g + 1) * HALF].bitcast(FP8),
                    func=ACT.Copy,
                    scale=scale_sb[:, c, j : j + 1],
                )

        def group_permuted(engine, name, c, g, columns=slice(0, P)):
            key = ("weights", name, c, g)
            if key not in grouped:
                new_grouped(key)
            out_view = grouped[key][:].rearrange("p (t m j) -> p m t j", t=BLOCKS, j=PACK)
            in_view = weights[name, c, g].rearrange("p j (m t) -> p m t j", t=BLOCKS)
            copy(engine, out_view[:, columns], in_view[:, columns])

        def group_plain(engine, name, c, d):
            out_view = new_grouped(("weights", name, c, d))[:].rearrange("p (q i j) -> p q j i", i=4, j=PACK)
            copy(engine, out_view, weights[name, c, d].rearrange("p j (q i) -> p q j i", i=4))

        permuted_banks = {}

        def permute_on_tensor(name, c, g):
            in_view = weights[name, c, g].rearrange("p j (m t) -> p t m j", t=BLOCKS)
            for half in range(2):
                bank = psum.tile([P, 2, P, PACK], BF16, name="bank", tag="bank")
                permuted_banks[name, c, g, half] = bank
                for q in range(2):
                    nc.tensor.matmul(
                        bank[:, q], lhsT=identity_bf16[:], rhs=in_view[:, 2 * half + q], start=True, stop=True
                    )

        def empty_permuted(engine, name, c, g):
            tile = new_grouped(("weights", name, c, g))
            width = PACK * HALF // 2
            for half in range(2):
                bank = permuted_banks[name, c, g, half][:].rearrange("p q m j -> p (q m j)")
                copy(engine, tile[:, half * width : (half + 1) * width], bank)


        silu = {}
        PASSES = (("recv", 0), ("share", 0), ("recv", 1), ("share", 1))

        def hidden(g, h):
            silu[g, h] = silu_pool.tile([P, HALF, PACK], F32, name="silu", tag="silu")
            for b in range(BLOCKS):
                tokens = slice(b * P, (b + 1) * P)
                bank = psum.tile([P, BLOCKS, P], F32, name="bank", tag="bank")
                for t in range(BLOCKS):
                    channels = slice(t * P, (t + 1) * P)
                    for name, c in PASSES:
                        weight_key, key_key = ("weights", name, c, g), ("keys", name, c, h)
                        nc.tensor.matmul_mx(
                            out=bank[:, t],
                            lhsT=codes[weight_key][:, channels].bitcast(FP8X4),
                            lhsT_scale=scales[weight_key][:, channels],
                            rhs=codes[key_key][:, tokens].bitcast(FP8X4),
                            rhs_scale=scales[key_key][:, tokens],
                            start=(name, c) == PASSES[0],
                            stop=(name, c) == PASSES[-1],
                        )
                nc.scalar.activation(
                    out=silu[g, h][:, tokens, :], in_=bank[:].rearrange("p t n -> p n t"), func=ACT.Silu
                )

        def gain(g, h):
            nc.vector.tensor_tensor(
                out=new_grouped(("hidden", g, h))[:].rearrange("p (n t) -> p n t", t=PACK),
                in0=silu[g, h][:],
                in1=gain_sb[:, g : g + 1, :].to_broadcast([P, HALF, PACK]),
                op=ALU.mult,
            )


        sums, tanh, gates, products = {}, {}, {}, {}

        def contract_hidden(name, h, d, b):
            tokens = slice(b * P, (b + 1) * P)
            sums[name, h, d, b] = psum.tile([P, HALF], F32, name="bank", tag="bank")
            for c in range(2):
                nc.tensor.matmul_mx(
                    out=sums[name, h, d, b][:],
                    lhsT=codes["hidden", c, h][:, tokens].bitcast(FP8X4),
                    lhsT_scale=scales["hidden", c, h][:, tokens],
                    rhs=codes["weights", name, c, d][:].bitcast(FP8X4),
                    rhs_scale=scales["weights", name, c, d][:],
                    start=(c == 0),
                    stop=(c == 1),
                )

        def on_gpsimd(h, d, b):
            return b == 1 and (h, d) != (0, 0)

        def gate(h, d, b):
            tanh[h, d, b] = gate_pool.tile([P, HALF], F32, name="gate", tag="gate")
            nc.scalar.activation(out=tanh[h, d, b][:], in_=sums["gate", h, d, b][:], func=ACT.Tanh, scale=0.5)
            if on_gpsimd(h, d, b):
                gates[h, d, b] = gate_pool.tile([P, HALF], F32, name="gate", tag="gate")
                nc.scalar.activation(
                    out=gates[h, d, b][:], in_=tanh[h, d, b][:], func=ACT.Identity, scale=0.5, bias=0.5
                )

        def product(h, d, b):
            products[h, d, b] = gate_pool.tile([P, HALF], F32, name="product", tag="product")
            delta = sums["delta", h, d, b][:]
            if on_gpsimd(h, d, b):
                nc.vector.tensor_tensor(out=products[h, d, b][:], in0=delta, in1=gates[h, d, b][:], op=ALU.mult)
            else:
                nc.vector.scalar_tensor_tensor(
                    out=products[h, d, b][:], in0=tanh[h, d, b][:], scalar=1.0, in1=delta, op0=ALU.add, op1=ALU.mult
                )

        def residual(h, d, b):
            result = out_pool.tile([P, HALF], F32, name="result", tag="result")
            columns = slice(d * HALF, (d + 1) * HALF)
            recv = keys["recv", h, b // 2][:, b % 2, columns]
            if on_gpsimd(h, d, b):
                nc.gpsimd.tensor_tensor(out=result[:], in0=products[h, d, b][:], in1=recv, op=ALU.add)
            else:
                nc.vector.scalar_tensor_tensor(
                    out=result[:], in0=products[h, d, b][:], scalar=0.5, in1=recv, op0=ALU.mult, op1=ALU.add
                )
            first = h * HALF + b * P
            nc.sync.dma_start(out=out[first : first + P, columns], in_=result[:])


        V, S = nc.vector, nc.scalar
        everything = slice(0, HALF)

        load_recv_weights(0, 0, slice(0, 256))
        load_share_bytes(0, slice(0, 2))
        load_recv_weights(0, 0, slice(256, 512))
        load_share_bytes(0, slice(2, 4))
        load_recv_weights(1, 0, everything)
        for i in range(2):
            load_keys("recv", 0, i)
            load_keys("share", 0, i)
        load_share_bytes(1, slice(0, 4))
        for c in range(2):
            load_recv_weights(c, 1, everything)
        for name in ("recv", "share"):
            for i in range(2):
                load_keys(name, 1, i)
        for c in range(2):
            for name in ("delta", "gate"):
                load_stage2_weights(name, c)

        group_permuted(V, "recv", 0, 0, columns=slice(0, 64))
        group_permuted(V, "recv", 0, 0, columns=slice(64, 128))
        widen(0, 0)
        quantize("weights", "recv", 0, 0)
        group_permuted(S, "share", 0, 0)
        permute_on_tensor("recv", 1, 0)
        empty_permuted(V, "recv", 1, 0)
        widen(0, 1)
        for i in range(2):
            transpose_keys("recv", 0, i)
            transpose_keys("share", 0, i)
        quantize("weights", "share", 0, 0)
        quantize("weights", "recv", 1, 0)
        for c in range(2):
            group_keys(V, "recv", c, 0, 0)
            group_keys(S, "share", c, 0, 0)
        group_keys(V, "recv", 1, 0, 1)
        group_keys(S, "recv", 0, 0, 1)
        quantize("keys", "recv", 1, 0)
        group_keys(V, "share", 1, 0, 1)
        widen(1, 0)
        group_keys(S, "share", 0, 0, 1)
        quantize("keys", "recv", 0, 0)
        quantize("keys", "share", 1, 0)

        group_permuted(V, "recv", 0, 1)
        quantize("keys", "share", 0, 0)
        widen(1, 1)
        group_permuted(V, "share", 1, 0)
        permute_on_tensor("recv", 1, 1)
        empty_permuted(S, "recv", 1, 1)
        quantize("weights", "recv", 0, 1)
        group_permuted(V, "share", 1, 1)
        quantize("weights", "share", 1, 0)
        quantize("weights", "share", 1, 1)
        for name in ("recv", "share"):
            for i in range(2):
                transpose_keys(name, 1, i)
                for c in range(2):
                    group_keys(S, name, c, 1, i)
        group_permuted(S, "share", 0, 1)
        quantize("keys", "recv", 0, 1)
        quantize("keys", "recv", 1, 1)
        quantize("weights", "recv", 1, 1)
        group_plain(V, "delta", 0, 1)
        quantize("keys", "share", 0, 1)
        quantize("keys", "share", 1, 1)
        quantize("weights", "delta", 0, 1)
        quantize("weights", "share", 0, 1)
        group_plain(V, "gate", 0, 1)

        hidden(0, 0)
        group_plain(S, "delta", 0, 0)
        gain(0, 0)
        group_plain(V, "delta", 1, 0)
        quantize("hidden", 0, 0)
        quantize("weights", "delta", 0, 0)
        quantize("weights", "gate", 0, 1)
        quantize("weights", "delta", 1, 0)
        group_plain(V, "gate", 1, 1)
        hidden(0, 1)
        group_plain(S, "gate", 1, 0)
        gain(0, 1)
        hidden(1, 0)
        group_plain(S, "gate", 0, 0)
        gain(1, 0)
        quantize("weights", "gate", 1, 0)
        quantize("weights", "gate", 0, 0)
        quantize("hidden", 1, 0)
        quantize("hidden", 0, 1)
        quantize("weights", "gate", 1, 1)
        hidden(1, 1)
        gain(1, 1)

        steps = [(h, d, b) for d in range(2) for h in range(2) for b in range(BLOCKS)]
        for n, step in enumerate(steps):
            contract_hidden("gate", *step)
            contract_hidden("delta", *step)
            gate(*step)
            product(*step)
            if n == 0:
                quantize("hidden", 1, 1)
            if n == 2:
                group_plain(S, "delta", 1, 1)
            if n == 5:
                quantize("weights", "delta", 1, 1)
            if n > 0:
                residual(*steps[n - 1])
        residual(*steps[-1])
